import numpy as np
import ml_dtypes


def mxq(x, axis, fmt="e4m3"):
    dtype, down = {"e4m3": (ml_dtypes.float8_e4m3fn, 7), "e5m2": (ml_dtypes.float8_e5m2, 14)}[fmt]
    v = np.moveaxis(np.asarray(x, np.float32).astype(ml_dtypes.bfloat16).astype(np.float64), axis, -1)
    blocks = v.reshape(v.shape[:-1] + (-1, 32))
    amax = np.abs(blocks).max(-1, keepdims=True)
    byte = np.maximum(np.where(amax > 0, np.frexp(amax)[1] - 1 + 127, 0) - down, 1)
    scale = np.exp2(byte - 127.0)
    codes = (blocks / scale).astype(np.float32).astype(dtype).astype(np.float64)
    return np.moveaxis((codes * scale).reshape(v.shape), -1, axis)


WIDE = False


def mx_kscale(k):
    if not WIDE:
        return np.ones(k)
    levels = np.array([10, -10, 5, -5, 0])
    if k % 512:
        return np.exp2(np.random.permutation(np.resize(levels, k // 32))).repeat(32)
    a = np.empty((k // 512, 16))
    for p in range(k // 512):
        a[p, :8] = np.random.permutation(np.resize(levels, 8))
        for g in range(8):
            far = levels[np.abs(levels - a[p, g]) >= 10]
            a[p, g + 8] = far[np.random.randint(len(far))]
    return np.exp2(a.ravel()).repeat(32)


def f64(x):
    return np.asarray(x).astype(np.float64)


def striped(idx):
    return np.tile(idx.reshape(-1, 16).T, (8, 1)).astype(np.uint16)


def unstriped(offs):
    return offs[:16].T.reshape(-1).astype(np.int64)


E2M1 = np.array([0.0, 0.5, 1.0, 1.5, 2.0, 3.0, 4.0, 6.0, -0.0, -0.5, -1.0, -1.5, -2.0, -3.0, -4.0, -6.0])


def pack_weight(w, fmt):
    k, n = w.shape
    w = f64(np.asarray(w, np.float32).astype(ml_dtypes.bfloat16)).reshape(k // 32, 32, n)
    amax = np.abs(w).max(1)
    if fmt == "e4m3":
        byte = np.frexp(amax)[1] - 1 + 127 - 7
    else:
        mant, ex = np.frexp(amax / 6.0)
        byte = np.where(mant > 0.5, ex, ex - 1) + 127
    byte = np.clip(np.where(amax > 0, byte, 1), 1, 254)
    scaled = (w * np.exp2(127.0 - byte)[:, None, :]).reshape(k, n).astype(np.float32)
    by_word = np.ascontiguousarray(scaled.reshape(k // 512, 128, 4, n).transpose(0, 1, 3, 2))
    if fmt == "e4m3":
        words = by_word.astype(ml_dtypes.float8_e4m3fn).view(np.uint8)
    else:
        c = by_word.astype(ml_dtypes.float4_e2m1fn).view(np.uint8) & 0xF
        words = (c[..., 0::2] | (c[..., 1::2] << 4)).reshape(k // 512, 128, 2 * n)
    return np.ascontiguousarray(words), np.ascontiguousarray(byte.astype(np.uint8).reshape(k // 512, 16, n))


def unpack_weight(words, scales, fmt):
    g, _, n = scales.shape
    words = np.ascontiguousarray(words).reshape(g, 128, n, -1)
    if fmt == "e4m3":
        vals = words.view(ml_dtypes.float8_e4m3fn).astype(np.float64)
    else:
        nib = np.empty((g, 128, n, 4), np.uint8)
        nib[..., 0::2] = words & 0xF
        nib[..., 1::2] = words >> 4
        vals = E2M1[nib]
    vals = vals * np.repeat(np.exp2(scales.astype(np.float64) - 127.0), 8, axis=1)[..., None]
    return vals.transpose(0, 1, 3, 2).reshape(g * 512, n)


def gelu(v):
    return 0.5 * v * (1.0 + np.tanh(np.sqrt(2.0 / np.pi) * (v + 0.044715 * v**3)))


K, T, S, H, T2, P, N = 512, 4096, 1024, 1536, 2048, 1024, 384

def setup_inputs():
    n = np.random.standard_normal
    s = mx_kscale(K)[:, None]
    u = mx_kscale(H)[:, None]
    tab_words, tab_scales = pack_weight(n((K, T)) * s, "e4m3")
    w1 = (n((K, H)) / np.sqrt(K) / s).astype(np.float32)
    w2_words, w2_scales = pack_weight(n((K, H)) / np.sqrt(K) / s, "e2m1")
    wgs = np.exp(0.3 * n((128, S))).astype(np.float32)
    prior = (np.exp(0.5 * n((H, P))) * u).astype(np.float32)
    w3 = (n((H, N)) / np.sqrt(H) / u).astype(np.float32)
    return {"tab_words": tab_words, "tab_scales": tab_scales,
            "offs": striped(np.random.permutation(T)[:S]),
            "offs2": striped(np.random.permutation(T2)[:S]),
            "offs3": striped(np.random.permutation(T2)[:P]),
            "w1": w1, "w2_words": w2_words, "w2_scales": w2_scales,
            "wgs": wgs, "prior": prior, "w3": w3}

def reference(tab_words, tab_scales, offs, offs2, offs3, w1, w2_words, w2_scales, wgs, prior, w3):
    v = unpack_weight(tab_words, tab_scales, "e4m3")[:, unstriped(offs)]
    w2 = unpack_weight(w2_words, w2_scales, "e2m1")
    timing = mxq(f64(w1), 0, "e4m3").T @ v
    volume = w2.T @ v
    h = np.maximum(timing, volume)
    page = np.zeros((H, T2))
    page[:, unstriped(offs2)] = np.tile(f64(wgs), (H // 128, 1)) * h
    x = page[:, unstriped(offs3)]
    pr = f64(prior)
    z = pr + pr * x
    return mxq(f64(w3), 0, "e4m3").T @ mxq(z, 0, "e4m3")

@@ -1,0 +1,335 @@
+from contextlib import ExitStack
+
+import concourse.mybir as mybir
+from concourse.masks import make_identity
+
+K, T, S, H, T2, M, N = 512, 4096, 1024, 1536, 2048, 1024, 384
+FLOPS = 2 * (2 * K * H * S + H * N * M)
+
+F32 = mybir.dt.float32
+BF16 = mybir.dt.bfloat16
+I32 = mybir.dt.int32
+U32 = mybir.dt.uint32
+U16 = mybir.dt.uint16
+U8 = mybir.dt.uint8
+E4M3 = mybir.dt.float8_e4m3fn_x4
+E2M1 = mybir.dt.float4_e2m1fn_x4
+MULT = mybir.AluOpType.mult
+MAX = mybir.AluOpType.max
+
+P = 128
+PACK = 4
+K_PASS = P * PACK
+BANK = 512
+SLICES = H // P
+GROUPS = H // K_PASS
+W1_CHUNKS = (128, 128, 256, 512, 512)
+TAIL_CHUNK = 256
+
+
+def tile_list_beacon_watch_scores_kernel(
+    tc, tab_words, tab_scales, offs, offs2, offs3, w1, w2_words, w2_scales, wgs, prior, w3, out
+):
+    nc = tc.nc
+    with ExitStack() as ctx:
+        keep = ctx.enter_context(tc.tile_pool(name="keep", bufs=1))
+        psum = ctx.enter_context(tc.psum_pool(name="psum", bufs=1))
+
+        banks = [psum.tile([P, BANK], F32, name=f"bank{b}") for b in range(8)]
+
+        idx = keep.tile([P, S // 16], U16)
+        idx2 = keep.tile([P, S // 16], U16)
+        idx3 = keep.tile([P, M // 16], U16)
+        table = keep.tile([P, T], I32, align_bytes=64)
+        table_scales = keep.tile([P, T], U8, align_bytes=64)
+        v_codes = keep.tile([P, S], U32, align_bytes=64)
+        v_scales = keep.tile([P, S], U8, align_bytes=64)
+        w1_codes = keep.tile([P, H], U32, align_bytes=64)
+        w1_scales = keep.tile([P, H], U8, align_bytes=64)
+        w2_plane = keep.tile([P, H], U8, align_bytes=64)
+        w3_codes = keep.tile([P, GROUPS * N], U32, align_bytes=64)
+        w3_scales = keep.tile([P, GROUPS * N], U8, align_bytes=64)
+        z_codes = keep.tile([P, GROUPS * M], U32, align_bytes=64)
+        z_scales = keep.tile([P, GROUPS * M], U8, align_bytes=64)
+        first_grouped = keep.tile([P, W1_CHUNKS[0] * PACK], BF16, align_bytes=64)
+        ident = keep.tile([P, P], F32)
+        pages = [keep.tile([P, T2], F32, name=f"page{i}") for i in range(2)]
+        timing = [keep.tile([P, S], F32, name=f"timing{i}") for i in range(2)]
+        evidence = [keep.tile([P, S], F32, name=f"evidence{i}") for i in range(2)]
+        change = [keep.tile([P, M], F32, name=f"change{i}") for i in range(2)]
+
+        def load_scale_rows(queue, plane, rows):
+            for q in range(4):
+                queue.dma_start(
+                    out=plane[:].bitcast(I32)[32 * q : 32 * q + 4, :],
+                    in_=rows[0, 4 * q : 4 * q + 4, :].bitcast(I32),
+                )
+
+        def load_into(raw, rows):
+            nc.sync.dma_start(out=raw[:], in_=rows.rearrange("(p j) c -> p j c", j=PACK))
+
+        def round_into(grouped, raw):
+            nc.scalar.copy(
+                out=grouped[:].rearrange("p (c i j) -> p c j i", i=4, j=PACK),
+                in_=raw[:].rearrange("p j (c i) -> p c j i", i=4),
+            )
+
+        nc.vector.memset(table_scales[:].bitcast(I32), 0)
+        nc.gpsimd.memset(w2_plane[:].bitcast(I32), 0)
+        load_scale_rows(nc.gpsimd, w2_plane, w2_scales)
+        nc.sync.dma_start(idx[:], offs)
+        with tc.tile_pool(name="head", bufs=1) as head:
+            first_raw = head.tile([P, PACK, W1_CHUNKS[0]], F32)
+            load_into(first_raw, w1[:, : W1_CHUNKS[0]])
+            nc.sync.dma_start(out=table[:], in_=tab_words[0].rearrange("p t i -> p (t i)").bitcast(I32))
+            load_scale_rows(nc.scalar, table_scales, tab_scales)
+            round_into(first_grouped, first_raw)
+        nc.sync.dma_start(idx2[:], offs2)
+        nc.sync.dma_start(idx3[:], offs3)
+
+        stage = ctx.enter_context(tc.tile_pool(name="stage", bufs=1))
+        w2_codes = stage.tile([P, 2 * H], U8, align_bytes=64)
+        weights = stage.tile([P, S], F32)
+        priors = [stage.tile([P, M], F32, name=f"prior{i}") for i in range(4)]
+
+        def load_rows(rows):
+            raw = stage.tile([P, PACK, rows.shape[1]], F32, name="raw", bufs=3)
+            load_into(raw, rows)
+            return raw
+
+        def round_rows(raw):
+            grouped = stage.tile([P, raw.shape[2] * PACK], BF16, name="grouped", align_bytes=64, bufs=2)
+            round_into(grouped, raw)
+            return grouped
+
+        def quantize(grouped, codes, scales, first, widths):
+            done = 0
+            for width in widths:
+                cols = slice(first + done, first + done + width)
+                nc.vector.quantize_mx(
+                    out=codes[:, cols].bitcast(E4M3),
+                    scales=scales[:, cols],
+                    in_=grouped[:, PACK * done : PACK * (done + width)],
+                )
+                done = done + width
+
+        w1_first = [sum(W1_CHUNKS[:c]) for c in range(len(W1_CHUNKS))]
+
+        def load_w1(c):
+            return load_rows(w1[:, w1_first[c] : w1_first[c] + W1_CHUNKS[c]])
+
+        def quantize_w1(c, raw):
+            quantize(round_rows(raw), w1_codes, w1_scales, w1_first[c], [W1_CHUNKS[c]])
+
+        def quantize_w3(g):
+            raw = load_rows(w3[g * K_PASS : (g + 1) * K_PASS, :])
+            quantize(round_rows(raw), w3_codes, w3_scales, g * N, [256, 128])
+
+        def load_prior(s):
+            nc.sync.dma_start(out=priors[s % 4][:], in_=prior[s * P : (s + 1) * P, :])
+
+        def detect(s, half):
+            cols = slice(half * BANK, (half + 1) * BANK)
+            rows = slice(s * P, (s + 1) * P)
+            nc.tensor.matmul_mx(
+                out=banks[half][:],
+                lhsT=w1_codes[:, rows].bitcast(E4M3),
+                lhsT_scale=w1_scales[:, rows],
+                rhs=v_codes[:, cols].bitcast(E4M3),
+                rhs_scale=v_scales[:, cols],
+                start=True,
+                stop=True,
+            )
+            nc.tensor.matmul_mx(
+                out=banks[2 + half][:],
+                lhsT=w2_codes[:, 2 * s * P : 2 * (s + 1) * P].bitcast(E2M1),
+                lhsT_scale=w2_plane[:, rows],
+                rhs=v_codes[:, cols].bitcast(E4M3),
+                rhs_scale=v_scales[:, cols],
+                start=True,
+                stop=True,
+            )
+            nc.scalar.copy(out=timing[s % 2][:, cols], in_=banks[half][:])
+
+        def stronger(s, half):
+            cols = slice(half * BANK, (half + 1) * BANK)
+            nc.vector.tensor_tensor(evidence[s % 2][:, cols], banks[2 + half][:], timing[s % 2][:, cols], MAX)
+
+        def scatter(s, first, width):
+            cols = slice(first, first + width)
+            nc.vector.tensor_tensor(
+                pages[s % 2][:].indirect(idx2[:, first // 16 : (first + width) // 16]),
+                evidence[s % 2][:, cols],
+                weights[:, cols],
+                MULT,
+            )
+
+        def gather(s, first, width):
+            cols = slice(first, first + width)
+            nc.vector.tensor_tensor(
+                change[s % 2][:, cols],
+                pages[s % 2][:].indirect(idx3[:, first // 16 : (first + width) // 16]),
+                priors[s % 4][:, cols],
+                MULT,
+            )
+
+        def turn_sum(s, first, width, bank):
+            blocks = width // P
+            for term, source in enumerate((priors[s % 4], change[s % 2])):
+                for b in range(blocks):
+                    nc.tensor.matmul(
+                        bank[:, b * P : (b + 1) * P],
+                        source[:, first + b * P : first + (b + 1) * P],
+                        ident[:],
+                        is_transpose=True,
+                        start=(term == 0 and b == 0),
+                        stop=(term == 1 and b == blocks - 1),
+                    )
+
+        def round_turned(s, bank_cols, turned):
+            place = s % PACK
+            nc.scalar.copy(
+                out=turned[:].rearrange("m (b u p e) -> m u b p e", u=2, p=P, e=2)[
+                    :, :, :, 32 * place : 32 * place + 32, :
+                ],
+                in_=bank_cols.rearrange("m (b p u e) -> m u b p e", p=32, u=2, e=2),
+            )
+
+        def turn_back(turned, first_block, bank, packed, engine_copy):
+            for b in range(2):
+                for u in range(2):
+                    at = (first_block + b) * K_PASS + u * 2 * P
+                    nc.tensor.transpose(
+                        bank[:, (2 * b + u) * P : (2 * b + u + 1) * P],
+                        turned[:, at : at + 2 * P].bitcast(F32),
+                        ident[:],
+                    )
+            engine_copy(
+                out=packed[:, first_block * K_PASS : (first_block + 2) * K_PASS]
+                .bitcast(F32)
+                .rearrange("p (b m u) -> p b m u", b=2, u=2),
+                in_=bank[:].rearrange("p (b u m) -> p b m u", b=2, u=2),
+            )
+
+        def score_pass(bank, nt, g, half, first, width, start, stop):
+            w_cols = slice(g * N + nt * P, g * N + (nt + 1) * P)
+            z_cols = slice(g * M + half * BANK + first, g * M + half * BANK + first + width)
+            nc.tensor.matmul_mx(
+                out=bank[:, first : first + width],
+                lhsT=w3_codes[:, w_cols].bitcast(E4M3),
+                lhsT_scale=w3_scales[:, w_cols],
+                rhs=z_codes[:, z_cols].bitcast(E4M3),
+                rhs_scale=z_scales[:, z_cols],
+                start=start,
+                stop=stop,
+            )
+
+        quantize(first_grouped, w1_codes, w1_scales, 0, [W1_CHUNKS[0]])
+        nc.sync.dma_start(out=w2_codes[:].bitcast(I32), in_=w2_words[0].bitcast(I32))
+        nc.sync.dma_start(out=weights[:], in_=wgs)
+        raw_second = load_w1(1)
+        load_prior(0)
+        make_identity(nc, ident[:])
+        for page in pages:
+            nc.vector.memset(page[:], 0.0)
+        for half in range(2):
+            nc.vector.tensor_copy(
+                v_scales[:, half * BANK : (half + 1) * BANK],
+                table_scales[:].indirect(idx[:, half * 32 : (half + 1) * 32]),
+            )
+            nc.vector.tensor_copy(
+                v_codes[:, half * BANK : (half + 1) * BANK],
+                table[:].bitcast(U32).indirect(idx[:, half * 32 : (half + 1) * 32]),
+            )
+        quantize_w1(1, raw_second)
+        for half in range(2):
+            detect(0, half)
+            stronger(0, half)
+
+        turned = {}
+        packed = {}
+        waiting = []
+        for s in range(SLICES):
+            g, place = divmod(s, PACK)
+            last = s == SLICES - 1
+            chunk = TAIL_CHUNK if g == GROUPS - 1 else BANK
+            if place == 0:
+                for c in range(M // chunk):
+                    tag = f"{chunk}_{c}"
+                    turned[g, c] = stage.tile([P, chunk * PACK], BF16, name="turned" + tag, align_bytes=64, bufs=1)
+                    packed[g, c] = stage.tile([P, chunk * PACK], BF16, name="packed" + tag, align_bytes=64, bufs=1)
+            if not last:
+                load_prior(s + 1)
+                for half in range(2):
+                    detect(s + 1, half)
+            if s == 0:
+                scatter(s, 0, BANK)
+                scatter(s, BANK, BANK)
+            else:
+                scatter(s, 0, S)
+            if not last:
+                for half in range(2):
+                    stronger(s + 1, half)
+            for job in waiting:
+                job()
+            waiting = []
+            if s + 2 in [first // P for first in w1_first[2:]]:
+                c = w1_first.index((s + 2) * P)
+                quantize_w1(c, load_w1(c))
+            if s in (3, 5, 7):
+                quantize_w3((s - 3) // 2)
+            if last:
+                break
+            gather(s, 0, M)
+            for half in range(2):
+                bank = banks[4 + half]
+                turn_sum(s, half * BANK, BANK, bank)
+                for c in range(BANK // chunk):
+                    round_turned(s, bank[:, c * chunk : (c + 1) * chunk], turned[g, half * (BANK // chunk) + c])
+            if place == PACK - 1:
+                for half in range(2):
+                    for pair in range(2):
+                        turn_back(turned[g, half], 2 * pair, banks[6 + pair], packed[g, half], nc.scalar.copy)
+                    waiting.append(
+                        lambda g=g, half=half: quantize(packed[g, half], z_codes, z_scales, g * M + half * BANK, [BANK])
+                    )
+
+        s, g = SLICES - 1, GROUPS - 1
+        sum_banks = (banks[3], banks[4], banks[5], banks[3])
+        back_banks = (banks[6], banks[7], banks[4], banks[5])
+        out_banks = ((banks[0], banks[1], banks[2]), (banks[6], banks[7], banks[3]))
+
+        def early_passes(half, nt):
+            for early in range(GROUPS - 1):
+                score_pass(out_banks[half][nt], nt, early, half, 0, BANK, early == 0, False)
+
+        def store(half):
+            for nt in range(N // P):
+                result = stage.tile([P, BANK], F32, name="result", bufs=6)
+                if nt == 1:
+                    nc.vector.tensor_copy(out=result[:], in_=out_banks[half][nt][:])
+                else:
+                    nc.scalar.copy(out=result[:], in_=out_banks[half][nt][:])
+                nc.sync.dma_start(out=out[nt * P : (nt + 1) * P, half * BANK : (half + 1) * BANK], in_=result[:])
+
+        for nt in range(N // P):
+            early_passes(0, nt)
+        chunks = M // TAIL_CHUNK
+        for c in range(chunks):
+            gather(s, c * TAIL_CHUNK, TAIL_CHUNK)
+        for c in range(chunks):
+            turn_sum(s, c * TAIL_CHUNK, TAIL_CHUNK, sum_banks[c])
+            round_turned(s, sum_banks[c][:, :TAIL_CHUNK], turned[g, c])
+            if c >= 1:
+                turn_back(turned[g, c - 1], 0, back_banks[c - 1], packed[g, c - 1], nc.scalar.copy)
+        turn_back(turned[g, chunks - 1], 0, back_banks[chunks - 1], packed[g, chunks - 1], nc.vector.tensor_copy)
+        for c in range(chunks):
+            half, part = divmod(c, 2)
+            quantize(packed[g, c], z_codes, z_scales, g * M + c * TAIL_CHUNK, [TAIL_CHUNK])
+            if c == 2:
+                for nt in range(N // P):
+                    early_passes(1, nt)
+            for nt in range(N // P):
+                score_pass(out_banks[half][nt], nt, g, half, part * TAIL_CHUNK, TAIL_CHUNK, False, part == 1)
+            if part == 1:
+                store(half)

@@ -15,7 +15,10 @@ U8 = mybir.dt.uint8
 E4M3 = mybir.dt.float8_e4m3fn_x4
 E2M1 = mybir.dt.float4_e2m1fn_x4
 MULT = mybir.AluOpType.mult
+ADD = mybir.AluOpType.add
 MAX = mybir.AluOpType.max
+COPY = mybir.ActivationFunctionType.Copy
+RELU = mybir.ActivationFunctionType.Relu
 
 P = 128
 PACK = 4
@@ -23,8 +26,19 @@ K_PASS = P * PACK
 BANK = 512
 SLICES = H // P
 GROUPS = H // K_PASS
-W1_CHUNKS = (128, 128, 256, 512, 512)
-TAIL_CHUNK = 256
+OUT_TILES = N // P
+LIST_ROWS = 16
+W1_CHUNKS = (128, 128, 256, 256, 256, 256, 256)
+W3_WIDTHS = (256, 128)
+MAIN_CHUNKS = (512, 512)
+TAIL_CHUNKS = (256, 256, 256, 128, 128)
+DIRECT_HALVES = {0: 2, 1: 2, 2: 1}
+PRIOR_BUFS = 4
+RAW_BUFS = 3
+
+
+def starts(widths):
+    return [sum(widths[:c]) for c in range(len(widths))]
 
 
 def tile_list_beacon_watch_scores_kernel(
@@ -37,9 +51,9 @@ def tile_list_beacon_watch_scores_kernel(
 
         banks = [psum.tile([P, BANK], F32, name=f"bank{b}") for b in range(8)]
 
-        idx = keep.tile([P, S // 16], U16)
-        idx2 = keep.tile([P, S // 16], U16)
-        idx3 = keep.tile([P, M // 16], U16)
+        idx = keep.tile([P, S // LIST_ROWS], U16)
+        idx2 = keep.tile([P, S // LIST_ROWS], U16)
+        idx3 = keep.tile([P, M // LIST_ROWS], U16)
         table = keep.tile([P, T], I32, align_bytes=64)
         table_scales = keep.tile([P, T], U8, align_bytes=64)
         v_codes = keep.tile([P, S], U32, align_bytes=64)
@@ -57,6 +71,9 @@ def tile_list_beacon_watch_scores_kernel(
         timing = [keep.tile([P, S], F32, name=f"timing{i}") for i in range(2)]
         evidence = [keep.tile([P, S], F32, name=f"evidence{i}") for i in range(2)]
         change = [keep.tile([P, M], F32, name=f"change{i}") for i in range(2)]
+        minus_volume = keep.tile([P, S], F32)
+        excess_t = [keep.tile([P, S], F32, name=f"excess_t{i}") for i in range(2)]
+        volume_t = [keep.tile([P, S], F32, name=f"volume_t{i}") for i in range(2)]
 
         def load_scale_rows(queue, plane, rows):
             for q in range(4):
@@ -90,43 +107,41 @@ def tile_list_beacon_watch_scores_kernel(
         stage = ctx.enter_context(tc.tile_pool(name="stage", bufs=1))
         w2_codes = stage.tile([P, 2 * H], U8, align_bytes=64)
         weights = stage.tile([P, S], F32)
-        priors = [stage.tile([P, M], F32, name=f"prior{i}") for i in range(4)]
+        priors = [stage.tile([P, M], F32, name=f"prior{i}") for i in range(PRIOR_BUFS)]
 
         def load_rows(rows):
-            raw = stage.tile([P, PACK, rows.shape[1]], F32, name="raw", bufs=3)
+            raw = stage.tile([P, PACK, rows.shape[1]], F32, name="raw", bufs=RAW_BUFS)
             load_into(raw, rows)
             return raw
 
-        def round_rows(raw):
-            grouped = stage.tile([P, raw.shape[2] * PACK], BF16, name="grouped", align_bytes=64, bufs=2)
+        def round_rows(raw, name):
+            grouped = stage.tile([P, raw.shape[2] * PACK], BF16, name=name, align_bytes=64)
             round_into(grouped, raw)
             return grouped
 
         def quantize(grouped, codes, scales, first, widths):
-            done = 0
-            for width in widths:
-                cols = slice(first + done, first + done + width)
+            for at, width in zip(starts(widths), widths):
+                cols = slice(first + at, first + at + width)
                 nc.vector.quantize_mx(
                     out=codes[:, cols].bitcast(E4M3),
                     scales=scales[:, cols],
-                    in_=grouped[:, PACK * done : PACK * (done + width)],
+                    in_=grouped[:, PACK * at : PACK * (at + width)],
                 )
-                done = done + width
 
-        w1_first = [sum(W1_CHUNKS[:c]) for c in range(len(W1_CHUNKS))]
+        w1_first = starts(W1_CHUNKS)
 
         def load_w1(c):
             return load_rows(w1[:, w1_first[c] : w1_first[c] + W1_CHUNKS[c]])
 
         def quantize_w1(c, raw):
-            quantize(round_rows(raw), w1_codes, w1_scales, w1_first[c], [W1_CHUNKS[c]])
+            quantize(round_rows(raw, f"w1_grouped{c}"), w1_codes, w1_scales, w1_first[c], [W1_CHUNKS[c]])
 
         def quantize_w3(g):
             raw = load_rows(w3[g * K_PASS : (g + 1) * K_PASS, :])
-            quantize(round_rows(raw), w3_codes, w3_scales, g * N, [256, 128])
+            quantize(round_rows(raw, f"w3_grouped{g}"), w3_codes, w3_scales, g * N, W3_WIDTHS)
 
         def load_prior(s):
-            nc.sync.dma_start(out=priors[s % 4][:], in_=prior[s * P : (s + 1) * P, :])
+            nc.sync.dma_start(out=priors[s % PRIOR_BUFS][:], in_=prior[s * P : (s + 1) * P, :])
 
         def detect(s, half):
             cols = slice(half * BANK, (half + 1) * BANK)
@@ -155,10 +170,39 @@ def tile_list_beacon_watch_scores_kernel(
             cols = slice(half * BANK, (half + 1) * BANK)
             nc.vector.tensor_tensor(evidence[s % 2][:, cols], banks[2 + half][:], timing[s % 2][:, cols], MAX)
 
+        def turn_add(bank_cols, sources):
+            blocks = sources[0].shape[1] // P
+            for term, source in enumerate(sources):
+                for b in range(blocks):
+                    nc.tensor.matmul(
+                        bank_cols[:, b * P : (b + 1) * P],
+                        source[:, b * P : (b + 1) * P],
+                        ident[:],
+                        is_transpose=True,
+                        start=(term == 0 and b == 0),
+                        stop=(term == len(sources) - 1 and b == blocks - 1),
+                    )
+
+        def excess_begin(s, half):
+            cols = slice(half * BANK, (half + 1) * BANK)
+            nc.scalar.activation(out=minus_volume[:, cols], in_=banks[2 + half][:], func=COPY, scale=-1.0)
+            turn_add(banks[half][:], [timing[s % 2][:, cols], minus_volume[:, cols]])
+            turn_add(banks[2 + half][:], [minus_volume[:, cols]])
+            nc.scalar.activation(out=excess_t[s % 2][:, cols], in_=banks[half][:], func=RELU)
+            nc.scalar.activation(out=volume_t[s % 2][:, cols], in_=banks[2 + half][:], func=COPY, scale=-1.0)
+
+        def excess_end(s, first):
+            width = (S - first) // 2
+            for part in range(2):
+                cols = slice(first + part * width, first + (part + 1) * width)
+                bank_cols = banks[4 + part][:, :width]
+                turn_add(bank_cols, [excess_t[s % 2][:, cols], volume_t[s % 2][:, cols]])
+                nc.scalar.copy(out=evidence[s % 2][:, cols], in_=bank_cols)
+
         def scatter(s, first, width):
             cols = slice(first, first + width)
             nc.vector.tensor_tensor(
-                pages[s % 2][:].indirect(idx2[:, first // 16 : (first + width) // 16]),
+                pages[s % 2][:].indirect(idx2[:, first // LIST_ROWS : (first + width) // LIST_ROWS]),
                 evidence[s % 2][:, cols],
                 weights[:, cols],
                 MULT,
@@ -168,23 +212,14 @@ def tile_list_beacon_watch_scores_kernel(
             cols = slice(first, first + width)
             nc.vector.tensor_tensor(
                 change[s % 2][:, cols],
-                pages[s % 2][:].indirect(idx3[:, first // 16 : (first + width) // 16]),
-                priors[s % 4][:, cols],
+                pages[s % 2][:].indirect(idx3[:, first // LIST_ROWS : (first + width) // LIST_ROWS]),
+                priors[s % PRIOR_BUFS][:, cols],
                 MULT,
             )
 
         def turn_sum(s, first, width, bank):
-            blocks = width // P
-            for term, source in enumerate((priors[s % 4], change[s % 2])):
-                for b in range(blocks):
-                    nc.tensor.matmul(
-                        bank[:, b * P : (b + 1) * P],
-                        source[:, first + b * P : first + (b + 1) * P],
-                        ident[:],
-                        is_transpose=True,
-                        start=(term == 0 and b == 0),
-                        stop=(term == 1 and b == blocks - 1),
-                    )
+            cols = slice(first, first + width)
+            turn_add(bank[:, :width], [priors[s % PRIOR_BUFS][:, cols], change[s % 2][:, cols]])
 
         def round_turned(s, bank_cols, turned):
             place = s % PACK
@@ -195,8 +230,8 @@ def tile_list_beacon_watch_scores_kernel(
                 in_=bank_cols.rearrange("m (b p u e) -> m u b p e", p=32, u=2, e=2),
             )
 
-        def turn_back(turned, first_block, bank, packed, engine_copy):
-            for b in range(2):
+        def turn_back(turned, first_block, blocks, bank, packed, engine_copy):
+            for b in range(blocks):
                 for u in range(2):
                     at = (first_block + b) * K_PASS + u * 2 * P
                     nc.tensor.transpose(
@@ -205,17 +240,17 @@ def tile_list_beacon_watch_scores_kernel(
                         ident[:],
                     )
             engine_copy(
-                out=packed[:, first_block * K_PASS : (first_block + 2) * K_PASS]
+                out=packed[:, first_block * K_PASS : (first_block + blocks) * K_PASS]
                 .bitcast(F32)
-                .rearrange("p (b m u) -> p b m u", b=2, u=2),
-                in_=bank[:].rearrange("p (b u m) -> p b m u", b=2, u=2),
+                .rearrange("p (b m u) -> p b m u", b=blocks, u=2),
+                in_=bank[:, : blocks * 2 * P].rearrange("p (b u m) -> p b m u", b=blocks, u=2),
             )
 
-        def score_pass(bank, nt, g, half, first, width, start, stop):
+        def score_pass(bank_cols, nt, g, first, start, stop):
             w_cols = slice(g * N + nt * P, g * N + (nt + 1) * P)
-            z_cols = slice(g * M + half * BANK + first, g * M + half * BANK + first + width)
+            z_cols = slice(g * M + first, g * M + first + bank_cols.shape[1])
             nc.tensor.matmul_mx(
-                out=bank[:, first : first + width],
+                out=bank_cols,
                 lhsT=w3_codes[:, w_cols].bitcast(E4M3),
                 lhsT_scale=w3_scales[:, w_cols],
                 rhs=z_codes[:, z_cols].bitcast(E4M3),
@@ -233,103 +268,117 @@ def tile_list_beacon_watch_scores_kernel(
         for page in pages:
             nc.vector.memset(page[:], 0.0)
         for half in range(2):
-            nc.vector.tensor_copy(
-                v_scales[:, half * BANK : (half + 1) * BANK],
-                table_scales[:].indirect(idx[:, half * 32 : (half + 1) * 32]),
-            )
-            nc.vector.tensor_copy(
-                v_codes[:, half * BANK : (half + 1) * BANK],
-                table[:].bitcast(U32).indirect(idx[:, half * 32 : (half + 1) * 32]),
-            )
+            entries = idx[:, half * BANK // LIST_ROWS : (half + 1) * BANK // LIST_ROWS]
+            cols = slice(half * BANK, (half + 1) * BANK)
+            nc.vector.tensor_copy(v_scales[:, cols], table_scales[:].indirect(entries))
+            nc.vector.tensor_copy(v_codes[:, cols], table[:].bitcast(U32).indirect(entries))
         quantize_w1(1, raw_second)
         for half in range(2):
             detect(0, half)
             stronger(0, half)
+            scatter(0, half * BANK, BANK)
+        for half in range(2):
+            detect(1, half)
+        quantize_w1(2, load_w1(2))
 
+        partial = stage.tile([P, OUT_TILES, BANK], F32)
         turned = {}
         packed = {}
-        waiting = []
         for s in range(SLICES):
             g, place = divmod(s, PACK)
             last = s == SLICES - 1
-            chunk = TAIL_CHUNK if g == GROUPS - 1 else BANK
+            widths = TAIL_CHUNKS if g == GROUPS - 1 else MAIN_CHUNKS
+            firsts = starts(widths)
             if place == 0:
-                for c in range(M // chunk):
-                    tag = f"{chunk}_{c}"
-                    turned[g, c] = stage.tile([P, chunk * PACK], BF16, name="turned" + tag, align_bytes=64, bufs=1)
-                    packed[g, c] = stage.tile([P, chunk * PACK], BF16, name="packed" + tag, align_bytes=64, bufs=1)
+                for c, chunk in enumerate(widths):
+                    tag = f"{len(widths)}_{c}"
+                    turned[g, c] = stage.tile([P, chunk * PACK], BF16, name="turned" + tag, align_bytes=64)
+                    packed[g, c] = stage.tile([P, chunk * PACK], BF16, name="packed" + tag, align_bytes=64)
             if not last:
                 load_prior(s + 1)
-                for half in range(2):
-                    detect(s + 1, half)
-            if s == 0:
-                scatter(s, 0, BANK)
-                scatter(s, BANK, BANK)
-            else:
+            if s > 0:
                 scatter(s, 0, S)
-            if not last:
+            for half in range(DIRECT_HALVES.get(s + 1, 0)):
+                stronger(s + 1, half)
+            if place == 0 and g > 0:
                 for half in range(2):
-                    stronger(s + 1, half)
-            for job in waiting:
-                job()
-            waiting = []
-            if s + 2 in [first // P for first in w1_first[2:]]:
-                c = w1_first.index((s + 2) * P)
+                    quantize(packed[g - 1, half], z_codes, z_scales, (g - 1) * M + half * BANK, [BANK])
+            if (s + 3) * P in w1_first:
+                c = w1_first.index((s + 3) * P)
                 quantize_w1(c, load_w1(c))
-            if s in (3, 5, 7):
+            ahead = s + 2
+            direct = DIRECT_HALVES.get(ahead, 0)
+            if ahead < SLICES:
+                for half in range(2):
+                    detect(ahead, half)
+                    if half >= direct:
+                        excess_begin(ahead, half)
+            if s % 2 == 1 and 0 <= (s - 3) // 2 < GROUPS:
                 quantize_w3((s - 3) // 2)
             if last:
                 break
+            if s == SLICES - 3:
+                for nt in range(OUT_TILES):
+                    bank = banks[6 + nt % 2]
+                    for early in range(GROUPS - 1):
+                        score_pass(bank[:], nt, early, BANK, early == 0, early == GROUPS - 2)
+                    nc.scalar.copy(out=partial[:, nt, :], in_=bank[:])
             gather(s, 0, M)
             for half in range(2):
                 bank = banks[4 + half]
                 turn_sum(s, half * BANK, BANK, bank)
-                for c in range(BANK // chunk):
-                    round_turned(s, bank[:, c * chunk : (c + 1) * chunk], turned[g, half * (BANK // chunk) + c])
+                for c, chunk in enumerate(widths):
+                    if firsts[c] // BANK == half:
+                        at = firsts[c] % BANK
+                        round_turned(s, bank[:, at : at + chunk], turned[g, c])
+            if ahead < SLICES:
+                excess_end(ahead, direct * BANK)
             if place == PACK - 1:
                 for half in range(2):
                     for pair in range(2):
-                        turn_back(turned[g, half], 2 * pair, banks[6 + pair], packed[g, half], nc.scalar.copy)
-                    waiting.append(
-                        lambda g=g, half=half: quantize(packed[g, half], z_codes, z_scales, g * M + half * BANK, [BANK])
-                    )
+                        turn_back(turned[g, half], 2 * pair, 2, banks[6 + pair], packed[g, half], nc.scalar.copy)
 
         s, g = SLICES - 1, GROUPS - 1
-        sum_banks = (banks[3], banks[4], banks[5], banks[3])
-        back_banks = (banks[6], banks[7], banks[4], banks[5])
-        out_banks = ((banks[0], banks[1], banks[2]), (banks[6], banks[7], banks[3]))
+        sum_banks = (banks[3], banks[4], banks[5], banks[4], banks[5])
+        back_banks = (banks[6], banks[7], banks[3], banks[6], banks[4])
+        back_copy = (nc.scalar.copy, nc.scalar.copy, nc.vector.tensor_copy, nc.scalar.copy, nc.scalar.copy)
+        out_rows = out.rearrange("(t p) m -> p t m", p=P)
 
-        def early_passes(half, nt):
+        for nt in range(OUT_TILES):
             for early in range(GROUPS - 1):
-                score_pass(out_banks[half][nt], nt, early, half, 0, BANK, early == 0, False)
+                score_pass(banks[nt][:], nt, early, 0, early == 0, False)
+        for c, chunk in enumerate(widths):
+            gather(s, firsts[c], chunk)
 
-        def store(half):
-            for nt in range(N // P):
-                result = stage.tile([P, BANK], F32, name="result", bufs=6)
-                if nt == 1:
-                    nc.vector.tensor_copy(out=result[:], in_=out_banks[half][nt][:])
-                else:
-                    nc.scalar.copy(out=result[:], in_=out_banks[half][nt][:])
-                nc.sync.dma_start(out=out[nt * P : (nt + 1) * P, half * BANK : (half + 1) * BANK], in_=result[:])
+        def finish(c):
+            first, chunk = firsts[c], widths[c]
+            turn_back(turned[g, c], 0, chunk // P, back_banks[c], packed[g, c], back_copy[c])
+            quantize(packed[g, c], z_codes, z_scales, g * M + first, [chunk])
+            if first < BANK:
+                for nt in range(OUT_TILES):
+                    score_pass(banks[nt][:, first : first + chunk], nt, g, first, False, first + chunk == BANK)
+                return
+            result = stage.tile([P, OUT_TILES, chunk], F32, name=f"result{c}")
+            fits = OUT_TILES * chunk <= BANK
+            runs = [(back_banks[c], 0, OUT_TILES)] if fits else [(banks[7], 0, 2), (back_banks[c], 2, 1)]
+            for bank, nt0, count in runs:
+                for i in range(count):
+                    score_pass(bank[:, i * chunk : (i + 1) * chunk], nt0 + i, g, first, True, True)
+                nc.vector.tensor_tensor(
+                    result[:, nt0 : nt0 + count, :],
+                    bank[:, : count * chunk].rearrange("p (t m) -> p t m", t=count),
+                    partial[:, nt0 : nt0 + count, first - BANK : first - BANK + chunk],
+                    ADD,
+                )
+            nc.sync.dma_start(out=out_rows[:, :, first : first + chunk], in_=result[:])
 
-        for nt in range(N // P):
-            early_passes(0, nt)
-        chunks = M // TAIL_CHUNK
-        for c in range(chunks):
-            gather(s, c * TAIL_CHUNK, TAIL_CHUNK)
-        for c in range(chunks):
-            turn_sum(s, c * TAIL_CHUNK, TAIL_CHUNK, sum_banks[c])
-            round_turned(s, sum_banks[c][:, :TAIL_CHUNK], turned[g, c])
+        for c, chunk in enumerate(widths):
+            turn_sum(s, firsts[c], chunk, sum_banks[c])
+            round_turned(s, sum_banks[c][:, :chunk], turned[g, c])
             if c >= 1:
-                turn_back(turned[g, c - 1], 0, back_banks[c - 1], packed[g, c - 1], nc.scalar.copy)
-        turn_back(turned[g, chunks - 1], 0, back_banks[chunks - 1], packed[g, chunks - 1], nc.vector.tensor_copy)
-        for c in range(chunks):
-            half, part = divmod(c, 2)
-            quantize(packed[g, c], z_codes, z_scales, g * M + c * TAIL_CHUNK, [TAIL_CHUNK])
-            if c == 2:
-                for nt in range(N // P):
-                    early_passes(1, nt)
-            for nt in range(N // P):
-                score_pass(out_banks[half][nt], nt, g, half, part * TAIL_CHUNK, TAIL_CHUNK, False, part == 1)
-            if part == 1:
-                store(half)
+                finish(c - 1)
+        finish(len(widths) - 1)
+        for nt in range(OUT_TILES):
+            first_half = stage.tile([P, BANK], F32, name="first_half", bufs=OUT_TILES)
+            nc.scalar.copy(out=first_half[:], in_=banks[nt][:])
+            nc.sync.dma_start(out=out_rows[:, nt, :BANK], in_=first_half[:])

@@ -32,7 +32,7 @@ W1_CHUNKS = (128, 128, 256, 256, 256, 256, 256)
 W3_WIDTHS = (256, 128)
 MAIN_CHUNKS = (512, 512)
 TAIL_CHUNKS = (256, 256, 256, 128, 128)
-DIRECT_HALVES = {0: 2, 1: 2, 2: 1}
+DIRECT_HALVES = {0: 2, 1: 2}
 PRIOR_BUFS = 4
 RAW_BUFS = 3
 
@@ -67,6 +67,7 @@ def tile_list_beacon_watch_scores_kernel(
         z_scales = keep.tile([P, GROUPS * M], U8, align_bytes=64)
         first_grouped = keep.tile([P, W1_CHUNKS[0] * PACK], BF16, align_bytes=64)
         ident = keep.tile([P, P], F32)
+        ident_bf = keep.tile([P, P], BF16)
         pages = [keep.tile([P, T2], F32, name=f"page{i}") for i in range(2)]
         timing = [keep.tile([P, S], F32, name=f"timing{i}") for i in range(2)]
         evidence = [keep.tile([P, S], F32, name=f"evidence{i}") for i in range(2)]
@@ -74,6 +75,8 @@ def tile_list_beacon_watch_scores_kernel(
         minus_volume = keep.tile([P, S], F32)
         excess_t = [keep.tile([P, S], F32, name=f"excess_t{i}") for i in range(2)]
         volume_t = [keep.tile([P, S], F32, name=f"volume_t{i}") for i in range(2)]
+
+        z_rows = [evidence[1 - i][:].bitcast(BF16) for i in range(2)]
 
         def load_scale_rows(queue, plane, rows):
             for q in range(4):
@@ -168,7 +171,8 @@ def tile_list_beacon_watch_scores_kernel(
 
         def stronger(s, half):
             cols = slice(half * BANK, (half + 1) * BANK)
-            nc.vector.tensor_tensor(evidence[s % 2][:, cols], banks[2 + half][:], timing[s % 2][:, cols], MAX)
+            target = change[1] if s == 0 else evidence[s % 2]
+            nc.vector.tensor_tensor(target[:, cols], banks[2 + half][:], timing[s % 2][:, cols], MAX)
 
         def turn_add(bank_cols, sources):
             blocks = sources[0].shape[1] // P
@@ -203,9 +207,45 @@ def tile_list_beacon_watch_scores_kernel(
             cols = slice(first, first + width)
             nc.vector.tensor_tensor(
                 pages[s % 2][:].indirect(idx2[:, first // LIST_ROWS : (first + width) // LIST_ROWS]),
-                evidence[s % 2][:, cols],
+                change[1][:, cols],
                 weights[:, cols],
                 MULT,
+            )
+
+        def weigh(s):
+            nc.gpsimd.tensor_tensor(change[s % 2][:], evidence[s % 2][:], weights[:], MULT)
+
+        def put(s):
+            nc.vector.tensor_copy(pages[s % 2][:].indirect(idx2[:]), change[s % 2][:])
+
+        def fetch(s, half):
+            cols = slice(half * BANK, (half + 1) * BANK)
+            nc.vector.tensor_scalar(
+                change[s % 2][:, cols],
+                pages[s % 2][:].indirect(idx3[:, half * BANK // LIST_ROWS : (half + 1) * BANK // LIST_ROWS]),
+                1.0,
+                1.0,
+                MULT,
+                ADD,
+            )
+            nc.gpsimd.tensor_tensor(
+                z_rows[s % 2][:, cols], change[s % 2][:, cols], priors[s % PRIOR_BUFS][:, cols], MULT
+            )
+
+        def turn_rows(s, half, bank):
+            for b in range(BANK // P):
+                at = half * BANK + b * P
+                nc.tensor.transpose(
+                    bank[:].bitcast(BF16)[:, b * P : (b + 1) * P], z_rows[s % 2][:, at : at + P], ident_bf[:]
+                )
+
+        def place_turned(s, bank_words, turned):
+            place = s % PACK
+            nc.scalar.copy(
+                out=turned[:].bitcast(F32).rearrange("m (b u p) -> m u b p", u=2, p=P)[
+                    :, :, :, 32 * place : 32 * place + 32
+                ],
+                in_=bank_words.rearrange("m (b p u) -> m u b p", p=32, u=2),
             )
 
         def gather(s, first, width):
@@ -265,6 +305,7 @@ def tile_list_beacon_watch_scores_kernel(
         raw_second = load_w1(1)
         load_prior(0)
         make_identity(nc, ident[:])
+        make_identity(nc, ident_bf[:])
         for page in pages:
             nc.vector.memset(page[:], 0.0)
         for half in range(2):
@@ -297,9 +338,11 @@ def tile_list_beacon_watch_scores_kernel(
             if not last:
                 load_prior(s + 1)
             if s > 0:
-                scatter(s, 0, S)
+                put(s)
             for half in range(DIRECT_HALVES.get(s + 1, 0)):
                 stronger(s + 1, half)
+            if not last:
+                weigh(s + 1)
             if place == 0 and g > 0:
                 for half in range(2):
                     quantize(packed[g - 1, half], z_codes, z_scales, (g - 1) * M + half * BANK, [BANK])
@@ -323,16 +366,17 @@ def tile_list_beacon_watch_scores_kernel(
                     for early in range(GROUPS - 1):
                         score_pass(bank[:], nt, early, BANK, early == 0, early == GROUPS - 2)
                     nc.scalar.copy(out=partial[:, nt, :], in_=bank[:])
-            gather(s, 0, M)
+            for half in range(2):
+                fetch(s, half)
+            if ahead < SLICES:
+                excess_end(ahead, direct * BANK)
             for half in range(2):
                 bank = banks[4 + half]
-                turn_sum(s, half * BANK, BANK, bank)
+                turn_rows(s, half, bank)
                 for c, chunk in enumerate(widths):
                     if firsts[c] // BANK == half:
                         at = firsts[c] % BANK
-                        round_turned(s, bank[:, at : at + chunk], turned[g, c])
-            if ahead < SLICES:
-                excess_end(ahead, direct * BANK)
+                        place_turned(s, bank[:, at // 2 : (at + chunk) // 2], turned[g, c])
             if place == PACK - 1:
                 for half in range(2):
                     for pair in range(2):

@@ -28,12 +28,14 @@ SLICES = H // P
 GROUPS = H // K_PASS
 OUT_TILES = N // P
 LIST_ROWS = 16
-W1_CHUNKS = (128, 128, 256, 256, 256, 256, 256)
-W3_WIDTHS = (256, 128)
+W1_CHUNKS = (128, 128, 256, 512, 256, 256)
+W3_CHUNKS = (512, 512, 128)
+W1_AFTER = {0: 4, 2: 5}
+W3_AFTER = {1: 0, 5: 1, 6: 2}
 MAIN_CHUNKS = (512, 512)
 TAIL_CHUNKS = (256, 256, 256, 128, 128)
-DIRECT_HALVES = {0: 2, 1: 2}
-PRIOR_BUFS = 4
+PAGES = 3
+PRIOR_BUFS = 3
 RAW_BUFS = 3
 
 
@@ -63,20 +65,19 @@ def tile_list_beacon_watch_scores_kernel(
         w2_plane = keep.tile([P, H], U8, align_bytes=64)
         w3_codes = keep.tile([P, GROUPS * N], U32, align_bytes=64)
         w3_scales = keep.tile([P, GROUPS * N], U8, align_bytes=64)
-        z_codes = keep.tile([P, GROUPS * M], U32, align_bytes=64)
         z_scales = keep.tile([P, GROUPS * M], U8, align_bytes=64)
         first_grouped = keep.tile([P, W1_CHUNKS[0] * PACK], BF16, align_bytes=64)
         ident = keep.tile([P, P], F32)
         ident_bf = keep.tile([P, P], BF16)
-        pages = [keep.tile([P, T2], F32, name=f"page{i}") for i in range(2)]
+        pages = [keep.tile([P, T2], F32, name=f"page{i}") for i in range(PAGES)]
         timing = [keep.tile([P, S], F32, name=f"timing{i}") for i in range(2)]
         evidence = [keep.tile([P, S], F32, name=f"evidence{i}") for i in range(2)]
-        change = [keep.tile([P, M], F32, name=f"change{i}") for i in range(2)]
+        weighted = [keep.tile([P, S], F32, name=f"weighted{i}") for i in range(2)]
         minus_volume = keep.tile([P, S], F32)
         excess_t = [keep.tile([P, S], F32, name=f"excess_t{i}") for i in range(2)]
         volume_t = [keep.tile([P, S], F32, name=f"volume_t{i}") for i in range(2)]
 
-        z_rows = [evidence[1 - i][:].bitcast(BF16) for i in range(2)]
+        change = evidence
 
         def load_scale_rows(queue, plane, rows):
             for q in range(4):
@@ -90,7 +91,7 @@ def tile_list_beacon_watch_scores_kernel(
 
         def round_into(grouped, raw):
             nc.scalar.copy(
-                out=grouped[:].rearrange("p (c i j) -> p c j i", i=4, j=PACK),
+                out=grouped.rearrange("p (c i j) -> p c j i", i=4, j=PACK),
                 in_=raw[:].rearrange("p j (c i) -> p c j i", i=4),
             )
 
@@ -103,48 +104,60 @@ def tile_list_beacon_watch_scores_kernel(
             load_into(first_raw, w1[:, : W1_CHUNKS[0]])
             nc.sync.dma_start(out=table[:], in_=tab_words[0].rearrange("p t i -> p (t i)").bitcast(I32))
             load_scale_rows(nc.scalar, table_scales, tab_scales)
-            round_into(first_grouped, first_raw)
-        nc.sync.dma_start(idx2[:], offs2)
-        nc.sync.dma_start(idx3[:], offs3)
+            round_into(first_grouped[:], first_raw)
 
         stage = ctx.enter_context(tc.tile_pool(name="stage", bufs=1))
         w2_codes = stage.tile([P, 2 * H], U8, align_bytes=64)
-        weights = stage.tile([P, S], F32)
-        priors = [stage.tile([P, M], F32, name=f"prior{i}") for i in range(PRIOR_BUFS)]
+        weights = stage.tile([P, S], F32, tag="weights", align_bytes=64)
+        priors = {}
+        z_codes = {}
+        z_rows = {}
+
+        def prior_place(s):
+            if s == PACK:
+                return "z_place"
+            return f"ring{s % PRIOR_BUFS}"
 
         def load_rows(rows):
             raw = stage.tile([P, PACK, rows.shape[1]], F32, name="raw", bufs=RAW_BUFS)
             load_into(raw, rows)
             return raw
 
-        def round_rows(raw, name):
-            grouped = stage.tile([P, raw.shape[2] * PACK], BF16, name=name, align_bytes=64)
-            round_into(grouped, raw)
-            return grouped
-
-        def quantize(grouped, codes, scales, first, widths):
-            for at, width in zip(starts(widths), widths):
-                cols = slice(first + at, first + at + width)
-                nc.vector.quantize_mx(
-                    out=codes[:, cols].bitcast(E4M3),
-                    scales=scales[:, cols],
-                    in_=grouped[:, PACK * at : PACK * (at + width)],
-                )
+        def quantize(grouped, codes, scales):
+            nc.vector.quantize_mx(out=codes.bitcast(E4M3), scales=scales, in_=grouped)
 
         w1_first = starts(W1_CHUNKS)
 
         def load_w1(c):
             return load_rows(w1[:, w1_first[c] : w1_first[c] + W1_CHUNKS[c]])
 
-        def quantize_w1(c, raw):
-            quantize(round_rows(raw, f"w1_grouped{c}"), w1_codes, w1_scales, w1_first[c], [W1_CHUNKS[c]])
+        def quantize_w1(c, raw, tag):
+            grouped = stage.tile([P, W1_CHUNKS[c] * PACK], BF16, name=f"w1_grouped{c}", tag=tag, align_bytes=64)
+            round_into(grouped[:], raw)
+            cols = slice(w1_first[c], w1_first[c] + W1_CHUNKS[c])
+            quantize(grouped[:], w1_codes[:, cols], w1_scales[:, cols])
 
-        def quantize_w3(g):
-            raw = load_rows(w3[g * K_PASS : (g + 1) * K_PASS, :])
-            quantize(round_rows(raw, f"w3_grouped{g}"), w3_codes, w3_scales, g * N, W3_WIDTHS)
+        w3_first = starts(W3_CHUNKS)
+
+        def quantize_w3(c, tag):
+            first, width = w3_first[c], W3_CHUNKS[c]
+            grouped = stage.tile([P, width * PACK], BF16, name=f"w3_grouped{c}", tag=tag, align_bytes=64)
+            for g in range(GROUPS):
+                lo, hi = max(first, g * N), min(first + width, (g + 1) * N)
+                if lo < hi:
+                    raw = load_rows(w3[g * K_PASS : (g + 1) * K_PASS, lo - g * N : hi - g * N])
+                    round_into(grouped[:, (lo - first) * PACK : (hi - first) * PACK], raw)
+            quantize(grouped[:], w3_codes[:, first : first + width], w3_scales[:, first : first + width])
+
+        def quantize_z(g, grouped, first, width):
+            quantize(grouped, z_codes[g][:, first : first + width], z_scales[:, g * M + first : g * M + first + width])
 
         def load_prior(s):
-            nc.sync.dma_start(out=priors[s % PRIOR_BUFS][:], in_=prior[s * P : (s + 1) * P, :])
+            if s == SLICES - 2:
+                priors[s] = volume_t[(SLICES - 1) % 2]
+            else:
+                priors[s] = stage.tile([P, M], F32, name=f"prior{s}", tag=prior_place(s), align_bytes=64)
+            nc.sync.dma_start(out=priors[s][:], in_=prior[s * P : (s + 1) * P, :])
 
         def detect(s, half):
             cols = slice(half * BANK, (half + 1) * BANK)
@@ -171,8 +184,7 @@ def tile_list_beacon_watch_scores_kernel(
 
         def stronger(s, half):
             cols = slice(half * BANK, (half + 1) * BANK)
-            target = change[1] if s == 0 else evidence[s % 2]
-            nc.vector.tensor_tensor(target[:, cols], banks[2 + half][:], timing[s % 2][:, cols], MAX)
+            nc.vector.tensor_tensor(evidence[s % 2][:, cols], banks[2 + half][:], timing[s % 2][:, cols], MAX)
 
         def turn_add(bank_cols, sources):
             blocks = sources[0].shape[1] // P
@@ -203,40 +215,35 @@ def tile_list_beacon_watch_scores_kernel(
                 turn_add(bank_cols, [excess_t[s % 2][:, cols], volume_t[s % 2][:, cols]])
                 nc.scalar.copy(out=evidence[s % 2][:, cols], in_=bank_cols)
 
-        def scatter(s, first, width):
+        def weigh(s, first, width):
             cols = slice(first, first + width)
-            nc.vector.tensor_tensor(
-                pages[s % 2][:].indirect(idx2[:, first // LIST_ROWS : (first + width) // LIST_ROWS]),
-                change[1][:, cols],
-                weights[:, cols],
-                MULT,
+            nc.gpsimd.tensor_tensor(weighted[s % 2][:, cols], evidence[s % 2][:, cols], weights[:, cols], MULT)
+
+        def put(s, first, width):
+            nc.vector.tensor_copy(
+                pages[s % PAGES][:].indirect(idx2[:, first // LIST_ROWS : (first + width) // LIST_ROWS]),
+                weighted[s % 2][:, first : first + width],
             )
-
-        def weigh(s):
-            nc.gpsimd.tensor_tensor(change[s % 2][:], evidence[s % 2][:], weights[:], MULT)
-
-        def put(s):
-            nc.vector.tensor_copy(pages[s % 2][:].indirect(idx2[:]), change[s % 2][:])
 
         def fetch(s, half):
             cols = slice(half * BANK, (half + 1) * BANK)
             nc.vector.tensor_scalar(
                 change[s % 2][:, cols],
-                pages[s % 2][:].indirect(idx3[:, half * BANK // LIST_ROWS : (half + 1) * BANK // LIST_ROWS]),
+                pages[s % PAGES][:].indirect(idx3[:, half * BANK // LIST_ROWS : (half + 1) * BANK // LIST_ROWS]),
                 1.0,
                 1.0,
                 MULT,
                 ADD,
             )
             nc.gpsimd.tensor_tensor(
-                z_rows[s % 2][:, cols], change[s % 2][:, cols], priors[s % PRIOR_BUFS][:, cols], MULT
+                z_rows[s][:, cols], change[s % 2][:, cols], priors[s][:, cols], MULT
             )
 
         def turn_rows(s, half, bank):
             for b in range(BANK // P):
                 at = half * BANK + b * P
                 nc.tensor.transpose(
-                    bank[:].bitcast(BF16)[:, b * P : (b + 1) * P], z_rows[s % 2][:, at : at + P], ident_bf[:]
+                    bank[:].bitcast(BF16)[:, b * P : (b + 1) * P], z_rows[s][:, at : at + P], ident_bf[:]
                 )
 
         def place_turned(s, bank_words, turned):
@@ -252,14 +259,14 @@ def tile_list_beacon_watch_scores_kernel(
             cols = slice(first, first + width)
             nc.vector.tensor_tensor(
                 change[s % 2][:, cols],
-                pages[s % 2][:].indirect(idx3[:, first // LIST_ROWS : (first + width) // LIST_ROWS]),
-                priors[s % PRIOR_BUFS][:, cols],
+                pages[s % PAGES][:].indirect(idx3[:, first // LIST_ROWS : (first + width) // LIST_ROWS]),
+                priors[s][:, cols],
                 MULT,
             )
 
         def turn_sum(s, first, width, bank):
             cols = slice(first, first + width)
-            turn_add(bank[:, :width], [priors[s % PRIOR_BUFS][:, cols], change[s % 2][:, cols]])
+            turn_add(bank[:, :width], [priors[s][:, cols], change[s % 2][:, cols]])
 
         def round_turned(s, bank_cols, turned):
             place = s % PACK
@@ -293,83 +300,72 @@ def tile_list_beacon_watch_scores_kernel(
                 out=bank_cols,
                 lhsT=w3_codes[:, w_cols].bitcast(E4M3),
                 lhsT_scale=w3_scales[:, w_cols],
-                rhs=z_codes[:, z_cols].bitcast(E4M3),
+                rhs=z_codes[g][:, first : first + bank_cols.shape[1]].bitcast(E4M3),
                 rhs_scale=z_scales[:, z_cols],
                 start=start,
                 stop=stop,
             )
 
-        quantize(first_grouped, w1_codes, w1_scales, 0, [W1_CHUNKS[0]])
+        quantize(first_grouped[:], w1_codes[:, : W1_CHUNKS[0]], w1_scales[:, : W1_CHUNKS[0]])
         nc.sync.dma_start(out=w2_codes[:].bitcast(I32), in_=w2_words[0].bitcast(I32))
-        nc.sync.dma_start(out=weights[:], in_=wgs)
         raw_second = load_w1(1)
-        load_prior(0)
+        raw_third = load_w1(2)
+        nc.sync.dma_start(out=weights[:], in_=wgs)
+        nc.sync.dma_start(idx2[:], offs2)
+        nc.sync.dma_start(idx3[:], offs3)
         make_identity(nc, ident[:])
         make_identity(nc, ident_bf[:])
-        for page in pages:
+        for page in pages[:-1]:
             nc.vector.memset(page[:], 0.0)
+        nc.gpsimd.memset(pages[-1][:], 0.0)
         for half in range(2):
             entries = idx[:, half * BANK // LIST_ROWS : (half + 1) * BANK // LIST_ROWS]
             cols = slice(half * BANK, (half + 1) * BANK)
             nc.vector.tensor_copy(v_scales[:, cols], table_scales[:].indirect(entries))
             nc.vector.tensor_copy(v_codes[:, cols], table[:].bitcast(U32).indirect(entries))
-        quantize_w1(1, raw_second)
+        quantize_w1(1, raw_second, "early1")
+        quantize_w1(2, raw_third, "early2")
         for half in range(2):
             detect(0, half)
             stronger(0, half)
-            scatter(0, half * BANK, BANK)
+            weigh(0, half * BANK, BANK)
+        put(0, 0, BANK)
         for half in range(2):
             detect(1, half)
-        quantize_w1(2, load_w1(2))
+            stronger(1, half)
+        weigh(1, 0, S)
+        put(0, BANK, BANK)
+        for half in range(2):
+            detect(2, half)
+            excess_begin(2, half)
+        excess_end(2, 0)
+        quantize_w1(3, load_w1(3), "early3")
 
         partial = stage.tile([P, OUT_TILES, BANK], F32)
         turned = {}
         packed = {}
-        for s in range(SLICES):
+
+        def fetch_slice(s):
+            z_rows[s] = stage.tile([P, M], BF16, name=f"z_rows{s}", tag=f"rows{s % 3}", align_bytes=64)
+            for half in range(2):
+                fetch(s, half)
+
+        def first_stage(s):
+            for half in range(2):
+                detect(s, half)
+                excess_begin(s, half)
+            excess_end(s, 0)
+
+        def second_stage(s):
             g, place = divmod(s, PACK)
-            last = s == SLICES - 1
             widths = TAIL_CHUNKS if g == GROUPS - 1 else MAIN_CHUNKS
             firsts = starts(widths)
             if place == 0:
                 for c, chunk in enumerate(widths):
                     tag = f"{len(widths)}_{c}"
                     turned[g, c] = stage.tile([P, chunk * PACK], BF16, name="turned" + tag, align_bytes=64)
-                    packed[g, c] = stage.tile([P, chunk * PACK], BF16, name="packed" + tag, align_bytes=64)
-            if not last:
-                load_prior(s + 1)
-            if s > 0:
-                put(s)
-            for half in range(DIRECT_HALVES.get(s + 1, 0)):
-                stronger(s + 1, half)
-            if not last:
-                weigh(s + 1)
-            if place == 0 and g > 0:
-                for half in range(2):
-                    quantize(packed[g - 1, half], z_codes, z_scales, (g - 1) * M + half * BANK, [BANK])
-            if (s + 3) * P in w1_first:
-                c = w1_first.index((s + 3) * P)
-                quantize_w1(c, load_w1(c))
-            ahead = s + 2
-            direct = DIRECT_HALVES.get(ahead, 0)
-            if ahead < SLICES:
-                for half in range(2):
-                    detect(ahead, half)
-                    if half >= direct:
-                        excess_begin(ahead, half)
-            if s % 2 == 1 and 0 <= (s - 3) // 2 < GROUPS:
-                quantize_w3((s - 3) // 2)
-            if last:
-                break
-            if s == SLICES - 3:
-                for nt in range(OUT_TILES):
-                    bank = banks[6 + nt % 2]
-                    for early in range(GROUPS - 1):
-                        score_pass(bank[:], nt, early, BANK, early == 0, early == GROUPS - 2)
-                    nc.scalar.copy(out=partial[:, nt, :], in_=bank[:])
-            for half in range(2):
-                fetch(s, half)
-            if ahead < SLICES:
-                excess_end(ahead, direct * BANK)
+                    if g == GROUPS - 1:
+                        packed[g, c] = stage.tile([P, chunk * PACK], BF16, name="packed" + tag, align_bytes=64)
             for half in range(2):
                 bank = banks[4 + half]
                 turn_rows(s, half, bank)
@@ -378,9 +374,47 @@ def tile_list_beacon_watch_scores_kernel(
                         at = firsts[c] % BANK
                         place_turned(s, bank[:, at // 2 : (at + chunk) // 2], turned[g, c])
             if place == PACK - 1:
+                packed[g] = stage.tile([P, M * PACK], BF16, name="packed", align_bytes=64)
                 for half in range(2):
+                    whole = packed[g][:, half * BANK * PACK : (half + 1) * BANK * PACK]
                     for pair in range(2):
-                        turn_back(turned[g, half], 2 * pair, 2, banks[6 + pair], packed[g, half], nc.scalar.copy)
+                        turn_back(turned[g, half], 2 * pair, 2, banks[6 + pair], whole, nc.scalar.copy)
+
+        load_prior(0)
+        first_stage(3)
+        for s in range(1, SLICES - 1):
+            load_prior(s)
+            put(s, 0, S)
+            weigh(s + 1, 0, S)
+            done, ahead = s - 1, s + 3
+            if s == SLICES - 2:
+                z_codes[1] = stage.tile([P, M], U32, name="z_codes1", tag="weights", align_bytes=64)
+                quantize_z(1, packed[1][:], 0, M)
+            fetch_slice(done)
+            if ahead < SLICES - 1:
+                first_stage(ahead)
+            second_stage(done)
+            if ahead == SLICES - 1:
+                first_stage(ahead)
+            if done in W1_AFTER:
+                quantize_w1(W1_AFTER[done], load_w1(W1_AFTER[done]), f"rows{done % 3}")
+            if done in W3_AFTER:
+                quantize_w3(W3_AFTER[done], f"rows{done % 3}")
+            if done == PACK:
+                z_codes[0] = stage.tile([P, M], U32, name="z_codes0", tag=prior_place(done), align_bytes=64)
+                quantize_z(0, packed[0][:], 0, M)
+        for nt in range(OUT_TILES):
+            bank = banks[6 + nt % 2]
+            for early in range(GROUPS - 1):
+                score_pass(bank[:], nt, early, BANK, early == 0, early == GROUPS - 2)
+            nc.scalar.copy(out=partial[:, nt, :], in_=bank[:])
+        z_codes[GROUPS - 1] = stage.tile([P, M], U32, name="z_codes_last", align_bytes=64)
+        load_prior(SLICES - 1)
+        fetch_slice(SLICES - 2)
+        second_stage(SLICES - 2)
+        put(SLICES - 1, 0, S)
+        widths = TAIL_CHUNKS
+        firsts = starts(widths)
 
         s, g = SLICES - 1, GROUPS - 1
         sum_banks = (banks[3], banks[4], banks[5], banks[4], banks[5])
@@ -397,7 +431,7 @@ def tile_list_beacon_watch_scores_kernel(
         def finish(c):
             first, chunk = firsts[c], widths[c]
             turn_back(turned[g, c], 0, chunk // P, back_banks[c], packed[g, c], back_copy[c])
-            quantize(packed[g, c], z_codes, z_scales, g * M + first, [chunk])
+            quantize_z(g, packed[g, c][:], first, chunk)
             if first < BANK:
                 for nt in range(OUT_TILES):
                     score_pass(banks[nt][:, first : first + chunk], nt, g, first, False, first + chunk == BANK)

@@ -17,6 +17,7 @@ E2M1 = mybir.dt.float4_e2m1fn_x4
 MULT = mybir.AluOpType.mult
 ADD = mybir.AluOpType.add
 MAX = mybir.AluOpType.max
+SUBTRACT = mybir.AluOpType.subtract
 COPY = mybir.ActivationFunctionType.Copy
 RELU = mybir.ActivationFunctionType.Relu
 
@@ -35,7 +36,7 @@ W3_AFTER = {1: 0, 5: 1, 6: 2}
 MAIN_CHUNKS = (512, 512)
 TAIL_CHUNKS = (256, 256, 256, 128, 128)
 PAGES = 3
-PRIOR_BUFS = 3
+RING = 5
 RAW_BUFS = 3
 
 
@@ -56,7 +57,7 @@ def tile_list_beacon_watch_scores_kernel(
         idx = keep.tile([P, S // LIST_ROWS], U16)
         idx2 = keep.tile([P, S // LIST_ROWS], U16)
         idx3 = keep.tile([P, M // LIST_ROWS], U16)
-        table = keep.tile([P, T], I32, align_bytes=64)
+        table = keep.tile([P, T], I32, tag="table", align_bytes=64)
         table_scales = keep.tile([P, T], U8, align_bytes=64)
         v_codes = keep.tile([P, S], U32, align_bytes=64)
         v_scales = keep.tile([P, S], U8, align_bytes=64)
@@ -68,16 +69,12 @@ def tile_list_beacon_watch_scores_kernel(
         z_scales = keep.tile([P, GROUPS * M], U8, align_bytes=64)
         first_grouped = keep.tile([P, W1_CHUNKS[0] * PACK], BF16, align_bytes=64)
         ident = keep.tile([P, P], F32)
-        ident_bf = keep.tile([P, P], BF16)
-        pages = [keep.tile([P, T2], F32, name=f"page{i}") for i in range(PAGES)]
+        pages = [keep.tile([P, T2], F32, name=f"page{i}") for i in range(PAGES - 1)]
         timing = [keep.tile([P, S], F32, name=f"timing{i}") for i in range(2)]
-        evidence = [keep.tile([P, S], F32, name=f"evidence{i}") for i in range(2)]
-        weighted = [keep.tile([P, S], F32, name=f"weighted{i}") for i in range(2)]
-        minus_volume = keep.tile([P, S], F32)
+        minus_volume = [keep.tile([P, S], F32, name=f"minus_volume{i}") for i in range(3)]
         excess_t = [keep.tile([P, S], F32, name=f"excess_t{i}") for i in range(2)]
-        volume_t = [keep.tile([P, S], F32, name=f"volume_t{i}") for i in range(2)]
-
-        change = evidence
+        excess = [keep.tile([P, S], F32, name=f"excess{i}") for i in range(2)]
+        weighted = [keep.tile([P, S], F32, name=f"weighted{i}") for i in range(2)]
 
         def load_scale_rows(queue, plane, rows):
             for q in range(4):
@@ -109,14 +106,10 @@ def tile_list_beacon_watch_scores_kernel(
         stage = ctx.enter_context(tc.tile_pool(name="stage", bufs=1))
         w2_codes = stage.tile([P, 2 * H], U8, align_bytes=64)
         weights = stage.tile([P, S], F32, tag="weights", align_bytes=64)
-        priors = {}
-        z_codes = {}
-        z_rows = {}
+        priors, evidence, change, z_codes = {}, {}, {}, {}
 
-        def prior_place(s):
-            if s == PACK:
-                return "z_place"
-            return f"ring{s % PRIOR_BUFS}"
+        def ring_tile(name, place, width=M, dtype=F32):
+            return stage.tile([P, width], dtype, name=name, tag=f"ring{place % RING}", align_bytes=64)
 
         def load_rows(rows):
             raw = stage.tile([P, PACK, rows.shape[1]], F32, name="raw", bufs=RAW_BUFS)
@@ -153,10 +146,7 @@ def tile_list_beacon_watch_scores_kernel(
             quantize(grouped, z_codes[g][:, first : first + width], z_scales[:, g * M + first : g * M + first + width])
 
         def load_prior(s):
-            if s == SLICES - 2:
-                priors[s] = volume_t[(SLICES - 1) % 2]
-            else:
-                priors[s] = stage.tile([P, M], F32, name=f"prior{s}", tag=prior_place(s), align_bytes=64)
+            priors[s] = ring_tile(f"prior{s}", s)
             nc.sync.dma_start(out=priors[s][:], in_=prior[s * P : (s + 1) * P, :])
 
         def detect(s, half):
@@ -184,7 +174,7 @@ def tile_list_beacon_watch_scores_kernel(
 
         def stronger(s, half):
             cols = slice(half * BANK, (half + 1) * BANK)
-            nc.vector.tensor_tensor(evidence[s % 2][:, cols], banks[2 + half][:], timing[s % 2][:, cols], MAX)
+            nc.vector.tensor_tensor(evidence[s][:, cols], banks[2 + half][:], timing[s % 2][:, cols], MAX)
 
         def turn_add(bank_cols, sources):
             blocks = sources[0].shape[1] // P
@@ -201,72 +191,55 @@ def tile_list_beacon_watch_scores_kernel(
 
         def excess_begin(s, half):
             cols = slice(half * BANK, (half + 1) * BANK)
-            nc.scalar.activation(out=minus_volume[:, cols], in_=banks[2 + half][:], func=COPY, scale=-1.0)
-            turn_add(banks[half][:], [timing[s % 2][:, cols], minus_volume[:, cols]])
-            turn_add(banks[2 + half][:], [minus_volume[:, cols]])
+            minus = minus_volume[s % 3][:, cols]
+            nc.scalar.activation(out=minus, in_=banks[2 + half][:], func=COPY, scale=-1.0)
+            turn_add(banks[half][:], [timing[s % 2][:, cols], minus])
             nc.scalar.activation(out=excess_t[s % 2][:, cols], in_=banks[half][:], func=RELU)
-            nc.scalar.activation(out=volume_t[s % 2][:, cols], in_=banks[2 + half][:], func=COPY, scale=-1.0)
 
-        def excess_end(s, first):
-            width = (S - first) // 2
-            for part in range(2):
-                cols = slice(first + part * width, first + (part + 1) * width)
-                bank_cols = banks[4 + part][:, :width]
-                turn_add(bank_cols, [excess_t[s % 2][:, cols], volume_t[s % 2][:, cols]])
-                nc.scalar.copy(out=evidence[s % 2][:, cols], in_=bank_cols)
+        def excess_end(s):
+            for half in range(2):
+                cols = slice(half * BANK, (half + 1) * BANK)
+                turn_add(banks[4 + half][:], [excess_t[s % 2][:, cols]])
+                nc.scalar.copy(out=excess[s % 2][:, cols], in_=banks[4 + half][:])
+
+        def add_volume(s):
+            evidence[s] = ring_tile(f"evidence{s}", s - 3)
+            nc.gpsimd.tensor_tensor(evidence[s][:], excess[s % 2][:], minus_volume[s % 3][:], SUBTRACT)
 
         def weigh(s, first, width):
             cols = slice(first, first + width)
-            nc.gpsimd.tensor_tensor(weighted[s % 2][:, cols], evidence[s % 2][:, cols], weights[:, cols], MULT)
+            nc.gpsimd.tensor_tensor(weighted[s % 2][:, cols], evidence[s][:, cols], weights[:, cols], MULT)
+
+        def places(s, first, width):
+            return pages[s % PAGES][:].indirect(idx2[:, first // LIST_ROWS : (first + width) // LIST_ROWS])
 
         def put(s, first, width):
-            nc.vector.tensor_copy(
-                pages[s % PAGES][:].indirect(idx2[:, first // LIST_ROWS : (first + width) // LIST_ROWS]),
-                weighted[s % 2][:, first : first + width],
-            )
-
-        def fetch(s, half):
-            cols = slice(half * BANK, (half + 1) * BANK)
-            nc.vector.tensor_scalar(
-                change[s % 2][:, cols],
-                pages[s % PAGES][:].indirect(idx3[:, half * BANK // LIST_ROWS : (half + 1) * BANK // LIST_ROWS]),
-                1.0,
-                1.0,
-                MULT,
-                ADD,
-            )
-            nc.gpsimd.tensor_tensor(
-                z_rows[s][:, cols], change[s % 2][:, cols], priors[s][:, cols], MULT
-            )
-
-        def turn_rows(s, half, bank):
-            for b in range(BANK // P):
-                at = half * BANK + b * P
-                nc.tensor.transpose(
-                    bank[:].bitcast(BF16)[:, b * P : (b + 1) * P], z_rows[s][:, at : at + P], ident_bf[:]
-                )
-
-        def place_turned(s, bank_words, turned):
-            place = s % PACK
-            nc.scalar.copy(
-                out=turned[:].bitcast(F32).rearrange("m (b u p) -> m u b p", u=2, p=P)[
-                    :, :, :, 32 * place : 32 * place + 32
-                ],
-                in_=bank_words.rearrange("m (b p u) -> m u b p", p=32, u=2),
-            )
+            nc.vector.tensor_copy(places(s, first, width), weighted[s % 2][:, first : first + width])
 
         def gather(s, first, width):
             cols = slice(first, first + width)
             nc.vector.tensor_tensor(
-                change[s % 2][:, cols],
+                change[s][:, cols],
                 pages[s % PAGES][:].indirect(idx3[:, first // LIST_ROWS : (first + width) // LIST_ROWS]),
                 priors[s][:, cols],
                 MULT,
             )
 
+        def turn_terms(bank_cols, source, start, stop):
+            blocks = source.shape[1] // P
+            for b in range(blocks):
+                nc.tensor.matmul(
+                    bank_cols[:, b * P : (b + 1) * P],
+                    source[:, b * P : (b + 1) * P],
+                    ident[:],
+                    is_transpose=True,
+                    start=(start and b == 0),
+                    stop=(stop and b == blocks - 1),
+                )
+
         def turn_sum(s, first, width, bank):
             cols = slice(first, first + width)
-            turn_add(bank[:, :width], [priors[s][:, cols], change[s % 2][:, cols]])
+            turn_add(bank[:, :width], [priors[s][:, cols], change[s][:, cols]])
 
         def round_turned(s, bank_cols, turned):
             place = s % PACK
@@ -314,47 +287,39 @@ def tile_list_beacon_watch_scores_kernel(
         nc.sync.dma_start(idx2[:], offs2)
         nc.sync.dma_start(idx3[:], offs3)
         make_identity(nc, ident[:])
-        make_identity(nc, ident_bf[:])
-        for page in pages[:-1]:
+        for page in pages:
             nc.vector.memset(page[:], 0.0)
-        nc.gpsimd.memset(pages[-1][:], 0.0)
         for half in range(2):
             entries = idx[:, half * BANK // LIST_ROWS : (half + 1) * BANK // LIST_ROWS]
             cols = slice(half * BANK, (half + 1) * BANK)
             nc.vector.tensor_copy(v_scales[:, cols], table_scales[:].indirect(entries))
             nc.vector.tensor_copy(v_codes[:, cols], table[:].bitcast(U32).indirect(entries))
+        last_page = keep.tile([P, T2], F32, tag="table", align_bytes=64)
+        nc.gpsimd.memset(last_page[:], 0.0)
+        pages.append(last_page)
         quantize_w1(1, raw_second, "early1")
         quantize_w1(2, raw_third, "early2")
+        for s in range(2):
+            evidence[s] = ring_tile(f"evidence{s}", s - 3)
         for half in range(2):
             detect(0, half)
             stronger(0, half)
-            weigh(0, half * BANK, BANK)
-        put(0, 0, BANK)
+        nc.vector.tensor_tensor(places(0, 0, BANK), evidence[0][:, :BANK], weights[:, :BANK], MULT)
+        weigh(0, BANK, BANK)
         for half in range(2):
             detect(1, half)
             stronger(1, half)
         weigh(1, 0, S)
         put(0, BANK, BANK)
-        for half in range(2):
-            detect(2, half)
-            excess_begin(2, half)
-        excess_end(2, 0)
-        quantize_w1(3, load_w1(3), "early3")
 
         partial = stage.tile([P, OUT_TILES, BANK], F32)
         turned = {}
         packed = {}
 
-        def fetch_slice(s):
-            z_rows[s] = stage.tile([P, M], BF16, name=f"z_rows{s}", tag=f"rows{s % 3}", align_bytes=64)
-            for half in range(2):
-                fetch(s, half)
-
-        def first_stage(s):
+        def first_stage_begin(s):
             for half in range(2):
                 detect(s, half)
                 excess_begin(s, half)
-            excess_end(s, 0)
 
         def second_stage(s):
             g, place = divmod(s, PACK)
@@ -367,12 +332,14 @@ def tile_list_beacon_watch_scores_kernel(
                     if g == GROUPS - 1:
                         packed[g, c] = stage.tile([P, chunk * PACK], BF16, name="packed" + tag, align_bytes=64)
             for half in range(2):
+                turn_terms(banks[4 + half][:], priors[s][:, half * BANK : (half + 1) * BANK], True, False)
+            for half in range(2):
                 bank = banks[4 + half]
-                turn_rows(s, half, bank)
+                turn_terms(bank[:], change[s][:, half * BANK : (half + 1) * BANK], False, True)
                 for c, chunk in enumerate(widths):
                     if firsts[c] // BANK == half:
                         at = firsts[c] % BANK
-                        place_turned(s, bank[:, at // 2 : (at + chunk) // 2], turned[g, c])
+                        round_turned(s, bank[:, at : at + chunk], turned[g, c])
             if place == PACK - 1:
                 packed[g] = stage.tile([P, M * PACK], BF16, name="packed", align_bytes=64)
                 for half in range(2):
@@ -380,39 +347,48 @@ def tile_list_beacon_watch_scores_kernel(
                     for pair in range(2):
                         turn_back(turned[g, half], 2 * pair, 2, banks[6 + pair], whole, nc.scalar.copy)
 
+        first_stage_begin(2)
+        excess_end(2)
+        add_volume(2)
+        weigh(2, 0, S)
         load_prior(0)
-        first_stage(3)
-        for s in range(1, SLICES - 1):
-            load_prior(s)
-            put(s, 0, S)
-            weigh(s + 1, 0, S)
-            done, ahead = s - 1, s + 3
-            if s == SLICES - 2:
+        quantize_w1(3, load_w1(3), "early3")
+        first_stage_begin(3)
+        excess_end(3)
+        load_prior(1)
+        for s in range(SLICES - 1):
+            if s + 1 < SLICES - 1:
+                put(s + 1, 0, S)
+            else:
                 z_codes[1] = stage.tile([P, M], U32, name="z_codes1", tag="weights", align_bytes=64)
                 quantize_z(1, packed[1][:], 0, M)
-            fetch_slice(done)
-            if ahead < SLICES - 1:
-                first_stage(ahead)
-            second_stage(done)
-            if ahead == SLICES - 1:
-                first_stage(ahead)
-            if done in W1_AFTER:
-                quantize_w1(W1_AFTER[done], load_w1(W1_AFTER[done]), f"rows{done % 3}")
-            if done in W3_AFTER:
-                quantize_w3(W3_AFTER[done], f"rows{done % 3}")
-            if done == PACK:
-                z_codes[0] = stage.tile([P, M], U32, name="z_codes0", tag=prior_place(done), align_bytes=64)
+            change[s] = ring_tile(f"change{s}", s - 2)
+            gather(s, 0, M)
+            if s + 4 < SLICES:
+                first_stage_begin(s + 4)
+            second_stage(s)
+            if s + 3 < SLICES:
+                add_volume(s + 3)
+                weigh(s + 3, 0, S)
+            if s + 4 < SLICES:
+                excess_end(s + 4)
+            if s in W1_AFTER:
+                quantize_w1(W1_AFTER[s], load_w1(W1_AFTER[s]), f"ring{(s - 2) % RING}")
+            if s in W3_AFTER:
+                quantize_w3(W3_AFTER[s], f"ring{(s - 2) % RING}")
+            if s == PACK - 1:
+                z_codes[0] = stage.tile([P, M], U32, name="z_codes0", align_bytes=64)
                 quantize_z(0, packed[0][:], 0, M)
+            if s + 2 < SLICES:
+                load_prior(s + 2)
         for nt in range(OUT_TILES):
             bank = banks[6 + nt % 2]
             for early in range(GROUPS - 1):
                 score_pass(bank[:], nt, early, BANK, early == 0, early == GROUPS - 2)
             nc.scalar.copy(out=partial[:, nt, :], in_=bank[:])
         z_codes[GROUPS - 1] = stage.tile([P, M], U32, name="z_codes_last", align_bytes=64)
-        load_prior(SLICES - 1)
-        fetch_slice(SLICES - 2)
-        second_stage(SLICES - 2)
         put(SLICES - 1, 0, S)
+        change[SLICES - 1] = ring_tile("change_last", SLICES - 3)
         widths = TAIL_CHUNKS
         firsts = starts(widths)
 

@@ -57,7 +57,7 @@ def tile_list_beacon_watch_scores_kernel(
         idx = keep.tile([P, S // LIST_ROWS], U16)
         idx2 = keep.tile([P, S // LIST_ROWS], U16)
         idx3 = keep.tile([P, M // LIST_ROWS], U16)
-        table = keep.tile([P, T], I32, tag="table", align_bytes=64)
+        table = keep.tile([P, T], I32, align_bytes=64)
         table_scales = keep.tile([P, T], U8, align_bytes=64)
         v_codes = keep.tile([P, S], U32, align_bytes=64)
         v_scales = keep.tile([P, S], U8, align_bytes=64)
@@ -69,12 +69,10 @@ def tile_list_beacon_watch_scores_kernel(
         z_scales = keep.tile([P, GROUPS * M], U8, align_bytes=64)
         first_grouped = keep.tile([P, W1_CHUNKS[0] * PACK], BF16, align_bytes=64)
         ident = keep.tile([P, P], F32)
-        pages = [keep.tile([P, T2], F32, name=f"page{i}") for i in range(PAGES - 1)]
+        pages = [keep.tile([P, T2], F32, name=f"page{i}") for i in range(PAGES)]
         timing = [keep.tile([P, S], F32, name=f"timing{i}") for i in range(2)]
-        minus_volume = [keep.tile([P, S], F32, name=f"minus_volume{i}") for i in range(3)]
-        excess_t = [keep.tile([P, S], F32, name=f"excess_t{i}") for i in range(2)]
-        excess = [keep.tile([P, S], F32, name=f"excess{i}") for i in range(2)]
-        weighted = [keep.tile([P, S], F32, name=f"weighted{i}") for i in range(2)]
+        minus_volume = keep.tile([P, S], F32)
+        evidence = [keep.tile([P, S], F32, name=f"evidence{i}") for i in range(3)]
 
         def load_scale_rows(queue, plane, rows):
             for q in range(4):
@@ -105,8 +103,8 @@ def tile_list_beacon_watch_scores_kernel(
 
         stage = ctx.enter_context(tc.tile_pool(name="stage", bufs=1))
         w2_codes = stage.tile([P, 2 * H], U8, align_bytes=64)
-        weights = stage.tile([P, S], F32, tag="weights", align_bytes=64)
-        priors, evidence, change, z_codes = {}, {}, {}, {}
+        weights = stage.tile([P, S], F32)
+        priors, change, z_codes, excess_t, volume_t = {}, {}, {}, {}, {}
 
         def ring_tile(name, place, width=M, dtype=F32):
             return stage.tile([P, width], dtype, name=name, tag=f"ring{place % RING}", align_bytes=64)
@@ -174,7 +172,7 @@ def tile_list_beacon_watch_scores_kernel(
 
         def stronger(s, half):
             cols = slice(half * BANK, (half + 1) * BANK)
-            nc.vector.tensor_tensor(evidence[s][:, cols], banks[2 + half][:], timing[s % 2][:, cols], MAX)
+            nc.vector.tensor_tensor(evidence[s % 3][:, cols], banks[2 + half][:], timing[s % 2][:, cols], MAX)
 
         def turn_add(bank_cols, sources):
             blocks = sources[0].shape[1] // P
@@ -191,30 +189,26 @@ def tile_list_beacon_watch_scores_kernel(
 
         def excess_begin(s, half):
             cols = slice(half * BANK, (half + 1) * BANK)
-            minus = minus_volume[s % 3][:, cols]
-            nc.scalar.activation(out=minus, in_=banks[2 + half][:], func=COPY, scale=-1.0)
-            turn_add(banks[half][:], [timing[s % 2][:, cols], minus])
-            nc.scalar.activation(out=excess_t[s % 2][:, cols], in_=banks[half][:], func=RELU)
+            nc.scalar.activation(out=minus_volume[:, cols], in_=banks[2 + half][:], func=COPY, scale=-1.0)
+            turn_add(banks[half][:], [timing[s % 2][:, cols], minus_volume[:, cols]])
+            turn_add(banks[2 + half][:], [minus_volume[:, cols]])
+            nc.scalar.activation(out=excess_t[s][:, cols], in_=banks[half][:], func=RELU)
+            nc.scalar.activation(out=volume_t[s][:, cols], in_=banks[2 + half][:], func=COPY, scale=-1.0)
 
         def excess_end(s):
             for half in range(2):
                 cols = slice(half * BANK, (half + 1) * BANK)
-                turn_add(banks[4 + half][:], [excess_t[s % 2][:, cols]])
-                nc.scalar.copy(out=excess[s % 2][:, cols], in_=banks[4 + half][:])
+                turn_add(banks[4 + half][:], [excess_t[s][:, cols], volume_t[s][:, cols]])
+                nc.scalar.copy(out=evidence[s % 3][:, cols], in_=banks[4 + half][:])
 
-        def add_volume(s):
-            evidence[s] = ring_tile(f"evidence{s}", s - 3)
-            nc.gpsimd.tensor_tensor(evidence[s][:], excess[s % 2][:], minus_volume[s % 3][:], SUBTRACT)
-
-        def weigh(s, first, width):
+        def scatter(s, first, width):
             cols = slice(first, first + width)
-            nc.gpsimd.tensor_tensor(weighted[s % 2][:, cols], evidence[s][:, cols], weights[:, cols], MULT)
-
-        def places(s, first, width):
-            return pages[s % PAGES][:].indirect(idx2[:, first // LIST_ROWS : (first + width) // LIST_ROWS])
-
-        def put(s, first, width):
-            nc.vector.tensor_copy(places(s, first, width), weighted[s % 2][:, first : first + width])
+            nc.vector.tensor_tensor(
+                pages[s % PAGES][:].indirect(idx2[:, first // LIST_ROWS : (first + width) // LIST_ROWS]),
+                evidence[s % 3][:, cols],
+                weights[:, cols],
+                MULT,
+            )
 
         def gather(s, first, width):
             cols = slice(first, first + width)
@@ -287,36 +281,32 @@ def tile_list_beacon_watch_scores_kernel(
         nc.sync.dma_start(idx2[:], offs2)
         nc.sync.dma_start(idx3[:], offs3)
         make_identity(nc, ident[:])
-        for page in pages:
+        for page in pages[:-1]:
             nc.vector.memset(page[:], 0.0)
+        nc.gpsimd.memset(pages[-1][:], 0.0)
         for half in range(2):
             entries = idx[:, half * BANK // LIST_ROWS : (half + 1) * BANK // LIST_ROWS]
             cols = slice(half * BANK, (half + 1) * BANK)
             nc.vector.tensor_copy(v_scales[:, cols], table_scales[:].indirect(entries))
             nc.vector.tensor_copy(v_codes[:, cols], table[:].bitcast(U32).indirect(entries))
-        last_page = keep.tile([P, T2], F32, tag="table", align_bytes=64)
-        nc.gpsimd.memset(last_page[:], 0.0)
-        pages.append(last_page)
         quantize_w1(1, raw_second, "early1")
         quantize_w1(2, raw_third, "early2")
-        for s in range(2):
-            evidence[s] = ring_tile(f"evidence{s}", s - 3)
         for half in range(2):
             detect(0, half)
             stronger(0, half)
-        nc.vector.tensor_tensor(places(0, 0, BANK), evidence[0][:, :BANK], weights[:, :BANK], MULT)
-        weigh(0, BANK, BANK)
+        scatter(0, 0, BANK)
         for half in range(2):
             detect(1, half)
             stronger(1, half)
-        weigh(1, 0, S)
-        put(0, BANK, BANK)
+        scatter(0, BANK, BANK)
 
         partial = stage.tile([P, OUT_TILES, BANK], F32)
         turned = {}
         packed = {}
 
         def first_stage_begin(s):
+            excess_t[s] = stage.tile([P, S], F32, name=f"excess_t{s}", tag=f"excess{s % 2}", align_bytes=64)
+            volume_t[s] = stage.tile([P, S], F32, name=f"volume_t{s}", tag=f"volume{s % 2}", align_bytes=64)
             for half in range(2):
                 detect(s, half)
                 excess_begin(s, half)
@@ -349,33 +339,28 @@ def tile_list_beacon_watch_scores_kernel(
 
         first_stage_begin(2)
         excess_end(2)
-        add_volume(2)
-        weigh(2, 0, S)
         load_prior(0)
         quantize_w1(3, load_w1(3), "early3")
         first_stage_begin(3)
-        excess_end(3)
         load_prior(1)
         for s in range(SLICES - 1):
             if s + 1 < SLICES - 1:
-                put(s + 1, 0, S)
+                scatter(s + 1, 0, S)
+                change[s] = ring_tile(f"change{s}", s - 2)
             else:
-                z_codes[1] = stage.tile([P, M], U32, name="z_codes1", tag="weights", align_bytes=64)
+                z_codes[1] = stage.tile([P, M], U32, name="z_codes1", tag="excess1", align_bytes=64)
                 quantize_z(1, packed[1][:], 0, M)
-            change[s] = ring_tile(f"change{s}", s - 2)
+                change[s] = stage.tile([P, M], F32, name=f"change{s}", tag="volume1", align_bytes=64)
             gather(s, 0, M)
+            if s + 3 < SLICES:
+                excess_end(s + 3)
             if s + 4 < SLICES:
                 first_stage_begin(s + 4)
             second_stage(s)
-            if s + 3 < SLICES:
-                add_volume(s + 3)
-                weigh(s + 3, 0, S)
-            if s + 4 < SLICES:
-                excess_end(s + 4)
             if s in W1_AFTER:
-                quantize_w1(W1_AFTER[s], load_w1(W1_AFTER[s]), f"ring{(s - 2) % RING}")
+                quantize_w1(W1_AFTER[s], load_w1(W1_AFTER[s]), f"late{s}")
             if s in W3_AFTER:
-                quantize_w3(W3_AFTER[s], f"ring{(s - 2) % RING}")
+                quantize_w3(W3_AFTER[s], f"late{s}")
             if s == PACK - 1:
                 z_codes[0] = stage.tile([P, M], U32, name="z_codes0", align_bytes=64)
                 quantize_z(0, packed[0][:], 0, M)
@@ -387,13 +372,14 @@ def tile_list_beacon_watch_scores_kernel(
                 score_pass(bank[:], nt, early, BANK, early == 0, early == GROUPS - 2)
             nc.scalar.copy(out=partial[:, nt, :], in_=bank[:])
         z_codes[GROUPS - 1] = stage.tile([P, M], U32, name="z_codes_last", align_bytes=64)
-        put(SLICES - 1, 0, S)
+        scatter(SLICES - 1, 0, S)
         change[SLICES - 1] = ring_tile("change_last", SLICES - 3)
         widths = TAIL_CHUNKS
         firsts = starts(widths)
 
         s, g = SLICES - 1, GROUPS - 1
-        sum_banks = (banks[3], banks[4], banks[5], banks[4], banks[5])
+        sum_at = (3, 4, 5, 4, 5)
+        sum_banks = [banks[b] for b in sum_at]
         back_banks = (banks[6], banks[7], banks[3], banks[6], banks[4])
         back_copy = (nc.scalar.copy, nc.scalar.copy, nc.vector.tensor_copy, nc.scalar.copy, nc.scalar.copy)
         out_rows = out.rearrange("(t p) m -> p t m", p=P)
@@ -401,6 +387,9 @@ def tile_list_beacon_watch_scores_kernel(
         for nt in range(OUT_TILES):
             for early in range(GROUPS - 1):
                 score_pass(banks[nt][:], nt, early, 0, early == 0, False)
+        early = len(set(sum_at))
+        for c in range(early):
+            turn_terms(sum_banks[c][:], priors[s][:, firsts[c] : firsts[c] + widths[c]], True, False)
         for c, chunk in enumerate(widths):
             gather(s, firsts[c], chunk)
 
@@ -427,7 +416,10 @@ def tile_list_beacon_watch_scores_kernel(
             nc.sync.dma_start(out=out_rows[:, :, first : first + chunk], in_=result[:])
 
         for c, chunk in enumerate(widths):
-            turn_sum(s, firsts[c], chunk, sum_banks[c])
+            cols = slice(firsts[c], firsts[c] + chunk)
+            if c >= early:
+                turn_terms(sum_banks[c][:], priors[s][:, cols], True, False)
+            turn_terms(sum_banks[c][:], change[s][:, cols], False, True)
             round_turned(s, sum_banks[c][:, :chunk], turned[g, c])
             if c >= 1:
                 finish(c - 1)

@@ -98,7 +98,11 @@ def tile_list_beacon_watch_scores_kernel(
             first_raw = head.tile([P, PACK, W1_CHUNKS[0]], F32)
             load_into(first_raw, w1[:, : W1_CHUNKS[0]])
             nc.sync.dma_start(out=table[:], in_=tab_words[0].rearrange("p t i -> p (t i)").bitcast(I32))
-            load_scale_rows(nc.scalar, table_scales, tab_scales)
+            for r in range(4):
+                nc.scalar.dma_start(
+                    out=table_scales[:].bitcast(I32)[r:P:32, :],
+                    in_=tab_scales[0].bitcast(I32)[r:16:4, :],
+                )
             round_into(first_grouped[:], first_raw)
 
         stage = ctx.enter_context(tc.tile_pool(name="stage", bufs=1))

@@ -28,6 +28,7 @@ BANK = 512
 SLICES = H // P
 GROUPS = H // K_PASS
 OUT_TILES = N // P
+SCALE_ROWS = K_PASS // 32
 LIST_ROWS = 16
 W1_CHUNKS = (128, 128, 256, 512, 256, 256)
 W3_CHUNKS = (512, 512, 128)
@@ -35,6 +36,7 @@ W1_AFTER = {0: 4, 2: 5}
 W3_AFTER = {1: 0, 5: 1, 6: 2}
 MAIN_CHUNKS = (512, 512)
 TAIL_CHUNKS = (256, 256, 256, 128, 128)
+LATE = 256
 PAGES = 3
 RING = 5
 RAW_BUFS = 3
@@ -57,8 +59,10 @@ def tile_list_beacon_watch_scores_kernel(
         idx = keep.tile([P, S // LIST_ROWS], U16)
         idx2 = keep.tile([P, S // LIST_ROWS], U16)
         idx3 = keep.tile([P, M // LIST_ROWS], U16)
-        table = keep.tile([P, T], I32, align_bytes=64)
-        table_scales = keep.tile([P, T], U8, align_bytes=64)
+        table = keep.tile([P, T], I32, tag="page2", align_bytes=64)
+        table_scales = keep.tile([P, T], U8, tag="page0", align_bytes=64)
+        w2_codes = keep.tile([P, 2 * H], U8, align_bytes=64)
+        weights = keep.tile([P, S], F32)
         v_codes = keep.tile([P, S], U32, align_bytes=64)
         v_scales = keep.tile([P, S], U8, align_bytes=64)
         w1_codes = keep.tile([P, H], U32, align_bytes=64)
@@ -69,7 +73,6 @@ def tile_list_beacon_watch_scores_kernel(
         z_scales = keep.tile([P, GROUPS * M], U8, align_bytes=64)
         first_grouped = keep.tile([P, W1_CHUNKS[0] * PACK], BF16, align_bytes=64)
         ident = keep.tile([P, P], F32)
-        pages = [keep.tile([P, T2], F32, name=f"page{i}") for i in range(PAGES)]
         timing = [keep.tile([P, S], F32, name=f"timing{i}") for i in range(2)]
         minus_volume = keep.tile([P, S], F32)
         evidence = [keep.tile([P, S], F32, name=f"evidence{i}") for i in range(3)]
@@ -90,24 +93,31 @@ def tile_list_beacon_watch_scores_kernel(
                 in_=raw[:].rearrange("p j (c i) -> p c j i", i=4),
             )
 
-        nc.vector.memset(table_scales[:].bitcast(I32), 0)
-        nc.gpsimd.memset(w2_plane[:].bitcast(I32), 0)
-        load_scale_rows(nc.gpsimd, w2_plane, w2_scales)
         nc.sync.dma_start(idx[:], offs)
         with tc.tile_pool(name="head", bufs=1) as head:
+            picked_scales = head.tile([P, S], U8, align_bytes=64)
+            nc.sync.dma_start(out=table_scales[:].bitcast(I32)[P - SCALE_ROWS :, :], in_=tab_scales[0].bitcast(I32))
             first_raw = head.tile([P, PACK, W1_CHUNKS[0]], F32)
             load_into(first_raw, w1[:, : W1_CHUNKS[0]])
             nc.sync.dma_start(out=table[:], in_=tab_words[0].rearrange("p t i -> p (t i)").bitcast(I32))
-            for r in range(4):
-                nc.scalar.dma_start(
-                    out=table_scales[:].bitcast(I32)[r:P:32, :],
-                    in_=tab_scales[0].bitcast(I32)[r:16:4, :],
-                )
+            nc.sync.dma_start(idx2[:], offs2)
+            nc.sync.dma_start(out=w2_codes[:].bitcast(I32), in_=w2_words[0].bitcast(I32))
+            nc.sync.dma_start(out=weights[:], in_=wgs)
+            nc.vector.memset(table_scales[:].bitcast(I32)[:96, :], 0)
+            nc.vector.memset(table_scales[:].bitcast(I32)[96 : P - SCALE_ROWS, :], 0)
+            nc.vector.memset(v_scales[:].bitcast(I32), 0)
+            nc.gpsimd.memset(w2_plane[:].bitcast(I32), 0)
+            load_scale_rows(nc.gpsimd, w2_plane, w2_scales)
+            nc.vector.tensor_copy(picked_scales[:], table_scales[:].indirect(idx[:]))
             round_into(first_grouped[:], first_raw)
+            for q in range(4):
+                first_row = P - SCALE_ROWS + 4 * q
+                nc.scalar.dma_start(
+                    out=v_scales[:].bitcast(I32)[32 * q : 32 * q + 4, :],
+                    in_=picked_scales[:].bitcast(I32)[first_row : first_row + 4, :],
+                )
 
         stage = ctx.enter_context(tc.tile_pool(name="stage", bufs=1))
-        w2_codes = stage.tile([P, 2 * H], U8, align_bytes=64)
-        weights = stage.tile([P, S], F32)
         priors, change, z_codes, excess_t, volume_t = {}, {}, {}, {}, {}
 
         def ring_tile(name, place, width=M, dtype=F32):
@@ -144,12 +154,30 @@ def tile_list_beacon_watch_scores_kernel(
                     round_into(grouped[:, (lo - first) * PACK : (hi - first) * PACK], raw)
             quantize(grouped[:], w3_codes[:, first : first + width], w3_scales[:, first : first + width])
 
+        def codes_of(g, first, width):
+            half, at = divmod(first, BANK)
+            if (g, half) in z_codes:
+                return z_codes[g, half][:, at : at + width]
+            return z_codes[g][:, first : first + width]
+
         def quantize_z(g, grouped, first, width):
-            quantize(grouped, z_codes[g][:, first : first + width], z_scales[:, g * M + first : g * M + first + width])
+            quantize(grouped, codes_of(g, first, width), z_scales[:, g * M + first : g * M + first + width])
 
         def load_prior(s):
+            if s == SLICES - 2:
+                for half, tag in enumerate((f"ring{s % RING}", "volume1")):
+                    priors[s, half] = stage.tile([P, BANK], F32, name=f"prior{s}_{half}", tag=tag, align_bytes=64)
+                    nc.sync.dma_start(
+                        out=priors[s, half][:], in_=prior[s * P : (s + 1) * P, half * BANK : (half + 1) * BANK]
+                    )
+                return
             priors[s] = ring_tile(f"prior{s}", s)
             nc.sync.dma_start(out=priors[s][:], in_=prior[s * P : (s + 1) * P, :])
+
+        def prior_of(s, first, width):
+            if s == SLICES - 2:
+                return priors[s, first // BANK][:, first % BANK : first % BANK + width]
+            return priors[s][:, first : first + width]
 
         def detect(s, half):
             cols = slice(half * BANK, (half + 1) * BANK)
@@ -200,16 +228,20 @@ def tile_list_beacon_watch_scores_kernel(
             nc.scalar.activation(out=volume_t[s][:, cols], in_=banks[2 + half][:], func=COPY, scale=-1.0)
 
         def excess_end(s):
+            last = S - LATE if s == SLICES - 1 else S
             for half in range(2):
-                cols = slice(half * BANK, (half + 1) * BANK)
-                turn_add(banks[4 + half][:], [excess_t[s][:, cols], volume_t[s][:, cols]])
-                nc.scalar.copy(out=evidence[s % 3][:, cols], in_=banks[4 + half][:])
+                cols = slice(half * BANK, min((half + 1) * BANK, last))
+                bank_cols = banks[4 + half][:, : cols.stop - cols.start]
+                turn_add(bank_cols, [excess_t[s][:, cols], volume_t[s][:, cols]])
+                nc.scalar.copy(out=evidence[s % 3][:, cols], in_=bank_cols)
+            if last < S:
+                turn_add(banks[3][:, :LATE], [excess_t[s][:, last:], volume_t[s][:, last:]])
 
-        def scatter(s, first, width):
+        def scatter(s, first, width, source=None):
             cols = slice(first, first + width)
             nc.vector.tensor_tensor(
                 pages[s % PAGES][:].indirect(idx2[:, first // LIST_ROWS : (first + width) // LIST_ROWS]),
-                evidence[s % 3][:, cols],
+                evidence[s % 3][:, cols] if source is None else source,
                 weights[:, cols],
                 MULT,
             )
@@ -219,7 +251,7 @@ def tile_list_beacon_watch_scores_kernel(
             nc.vector.tensor_tensor(
                 change[s][:, cols],
                 pages[s % PAGES][:].indirect(idx3[:, first // LIST_ROWS : (first + width) // LIST_ROWS]),
-                priors[s][:, cols],
+                prior_of(s, first, width),
                 MULT,
             )
 
@@ -271,28 +303,26 @@ def tile_list_beacon_watch_scores_kernel(
                 out=bank_cols,
                 lhsT=w3_codes[:, w_cols].bitcast(E4M3),
                 lhsT_scale=w3_scales[:, w_cols],
-                rhs=z_codes[g][:, first : first + bank_cols.shape[1]].bitcast(E4M3),
+                rhs=codes_of(g, first, bank_cols.shape[1]).bitcast(E4M3),
                 rhs_scale=z_scales[:, z_cols],
                 start=start,
                 stop=stop,
             )
 
         quantize(first_grouped[:], w1_codes[:, : W1_CHUNKS[0]], w1_scales[:, : W1_CHUNKS[0]])
-        nc.sync.dma_start(out=w2_codes[:].bitcast(I32), in_=w2_words[0].bitcast(I32))
         raw_second = load_w1(1)
         raw_third = load_w1(2)
-        nc.sync.dma_start(out=weights[:], in_=wgs)
-        nc.sync.dma_start(idx2[:], offs2)
         nc.sync.dma_start(idx3[:], offs3)
         make_identity(nc, ident[:])
-        for page in pages[:-1]:
-            nc.vector.memset(page[:], 0.0)
-        nc.gpsimd.memset(pages[-1][:], 0.0)
+        pages = [keep.tile([P, T2], F32, name=f"page{i}", tag=f"page{i}", align_bytes=64) for i in range(PAGES - 1)]
+        nc.vector.memset(pages[1][:], 0.0)
+        nc.vector.memset(pages[0][:], 0.0)
         for half in range(2):
             entries = idx[:, half * BANK // LIST_ROWS : (half + 1) * BANK // LIST_ROWS]
             cols = slice(half * BANK, (half + 1) * BANK)
-            nc.vector.tensor_copy(v_scales[:, cols], table_scales[:].indirect(entries))
             nc.vector.tensor_copy(v_codes[:, cols], table[:].bitcast(U32).indirect(entries))
+        pages.append(keep.tile([P, T2], F32, name="page2", tag="page2", align_bytes=64))
+        nc.gpsimd.memset(pages[2][:], 0.0)
         quantize_w1(1, raw_second, "early1")
         quantize_w1(2, raw_third, "early2")
         for half in range(2):
@@ -315,7 +345,7 @@ def tile_list_beacon_watch_scores_kernel(
                 detect(s, half)
                 excess_begin(s, half)
 
-        def second_stage(s):
+        def second_stage(s, between=None):
             g, place = divmod(s, PACK)
             widths = TAIL_CHUNKS if g == GROUPS - 1 else MAIN_CHUNKS
             firsts = starts(widths)
@@ -325,10 +355,13 @@ def tile_list_beacon_watch_scores_kernel(
                     turned[g, c] = stage.tile([P, chunk * PACK], BF16, name="turned" + tag, align_bytes=64)
                     if g == GROUPS - 1:
                         packed[g, c] = stage.tile([P, chunk * PACK], BF16, name="packed" + tag, align_bytes=64)
+            bank0 = 6 if s == SLICES - 2 else 4
             for half in range(2):
-                turn_terms(banks[4 + half][:], priors[s][:, half * BANK : (half + 1) * BANK], True, False)
+                turn_terms(banks[bank0 + half][:], prior_of(s, half * BANK, BANK), True, False)
+            if between is not None:
+                between()
             for half in range(2):
-                bank = banks[4 + half]
+                bank = banks[bank0 + half]
                 turn_terms(bank[:], change[s][:, half * BANK : (half + 1) * BANK], False, True)
                 for c, chunk in enumerate(widths):
                     if firsts[c] // BANK == half:
@@ -347,14 +380,9 @@ def tile_list_beacon_watch_scores_kernel(
         quantize_w1(3, load_w1(3), "early3")
         first_stage_begin(3)
         load_prior(1)
-        for s in range(SLICES - 1):
-            if s + 1 < SLICES - 1:
-                scatter(s + 1, 0, S)
-                change[s] = ring_tile(f"change{s}", s - 2)
-            else:
-                z_codes[1] = stage.tile([P, M], U32, name="z_codes1", tag="excess1", align_bytes=64)
-                quantize_z(1, packed[1][:], 0, M)
-                change[s] = stage.tile([P, M], F32, name=f"change{s}", tag="volume1", align_bytes=64)
+        for s in range(SLICES - 2):
+            scatter(s + 1, 0, S)
+            change[s] = ring_tile(f"change{s}", s - 2)
             gather(s, 0, M)
             if s + 3 < SLICES:
                 excess_end(s + 3)
@@ -370,13 +398,27 @@ def tile_list_beacon_watch_scores_kernel(
                 quantize_z(0, packed[0][:], 0, M)
             if s + 2 < SLICES:
                 load_prior(s + 2)
+        second_codes = stage.tile([P, BANK], U32, name="z_codes1", tag="excess1", align_bytes=64)
+        z_codes[1, 1] = second_codes[:]
+        quantize_z(1, packed[1][:, BANK * PACK :], BANK, BANK)
         for nt in range(OUT_TILES):
             bank = banks[6 + nt % 2]
             for early in range(GROUPS - 1):
                 score_pass(bank[:], nt, early, BANK, early == 0, early == GROUPS - 2)
             nc.scalar.copy(out=partial[:, nt, :], in_=bank[:])
         z_codes[GROUPS - 1] = stage.tile([P, M], U32, name="z_codes_last", align_bytes=64)
-        scatter(SLICES - 1, 0, S)
+        s = SLICES - 2
+        scatter(s + 1, 0, S - LATE)
+        change[s] = ring_tile(f"change{s}", s - 3)
+        gather(s, BANK, LATE)
+        gather(s, 0, BANK)
+        gather(s, BANK + LATE, BANK - LATE)
+        late = priors[s, 1][:, :LATE]
+        second_stage(s, lambda: nc.scalar.copy(out=late, in_=banks[3][:, :LATE]))
+        first_codes = stage.tile([P, BANK], U32, name="z_codes1_first", tag=f"ring{s % RING}", align_bytes=64)
+        z_codes[1, 0] = first_codes[:]
+        quantize_z(1, packed[1][:, : BANK * PACK], 0, BANK)
+        scatter(s + 1, S - LATE, LATE, late)
         change[SLICES - 1] = ring_tile("change_last", SLICES - 3)
         widths = TAIL_CHUNKS
         firsts = starts(widths)
@@ -388,12 +430,12 @@ def tile_list_beacon_watch_scores_kernel(
         back_copy = (nc.scalar.copy, nc.scalar.copy, nc.vector.tensor_copy, nc.scalar.copy, nc.scalar.copy)
         out_rows = out.rearrange("(t p) m -> p t m", p=P)
 
-        for nt in range(OUT_TILES):
-            for early in range(GROUPS - 1):
-                score_pass(banks[nt][:], nt, early, 0, early == 0, False)
         early = len(set(sum_at))
         for c in range(early):
             turn_terms(sum_banks[c][:], priors[s][:, firsts[c] : firsts[c] + widths[c]], True, False)
+        for nt in range(OUT_TILES):
+            for step in range(GROUPS - 1):
+                score_pass(banks[nt][:], nt, GROUPS - 2 - step, 0, step == 0, False)
         for c, chunk in enumerate(widths):
             gather(s, firsts[c], chunk)
 

@@ -59,7 +59,8 @@ def tile_list_beacon_watch_scores_kernel(
         idx = keep.tile([P, S // LIST_ROWS], U16)
         idx2 = keep.tile([P, S // LIST_ROWS], U16)
         idx3 = keep.tile([P, M // LIST_ROWS], U16)
-        table = keep.tile([P, T], I32, tag="page2", align_bytes=64)
+        table = keep.tile([P, T], I32, align_bytes=64)
+        first_evidence = keep.tile([P, S], F32, tag="page2", align_bytes=64)
         table_scales = keep.tile([P, T], U8, tag="page0", align_bytes=64)
         w2_codes = keep.tile([P, 2 * H], U8, align_bytes=64)
         weights = keep.tile([P, S], F32)
@@ -72,6 +73,8 @@ def tile_list_beacon_watch_scores_kernel(
         w3_scales = keep.tile([P, GROUPS * N], U8, align_bytes=64)
         z_scales = keep.tile([P, GROUPS * M], U8, align_bytes=64)
         first_grouped = keep.tile([P, W1_CHUNKS[0] * PACK], BF16, align_bytes=64)
+        raw_second = keep.tile([P, PACK, W1_CHUNKS[1]], F32)
+        second_grouped = keep.tile([P, W1_CHUNKS[1] * PACK], BF16, align_bytes=64)
         ident = keep.tile([P, P], F32)
         timing = [keep.tile([P, S], F32, name=f"timing{i}") for i in range(2)]
         minus_volume = keep.tile([P, S], F32)
@@ -99,9 +102,14 @@ def tile_list_beacon_watch_scores_kernel(
             nc.sync.dma_start(out=table_scales[:].bitcast(I32)[P - SCALE_ROWS :, :], in_=tab_scales[0].bitcast(I32))
             first_raw = head.tile([P, PACK, W1_CHUNKS[0]], F32)
             load_into(first_raw, w1[:, : W1_CHUNKS[0]])
-            nc.sync.dma_start(out=table[:], in_=tab_words[0].rearrange("p t i -> p (t i)").bitcast(I32))
+            w2_rows = w2_words[0].bitcast(I32)
+            first_words = P // 2
+            nc.sync.dma_start(out=w2_codes[:].bitcast(I32)[:, :first_words], in_=w2_rows[:, :first_words])
             nc.sync.dma_start(idx2[:], offs2)
-            nc.sync.dma_start(out=w2_codes[:].bitcast(I32), in_=w2_words[0].bitcast(I32))
+            nc.sync.dma_start(idx3[:], offs3)
+            nc.sync.dma_start(out=table[:], in_=tab_words[0].rearrange("p t i -> p (t i)").bitcast(I32))
+            nc.sync.dma_start(out=w2_codes[:].bitcast(I32)[:, first_words:], in_=w2_rows[:, first_words:])
+            load_into(raw_second, w1[:, W1_CHUNKS[0] : W1_CHUNKS[0] + W1_CHUNKS[1]])
             nc.sync.dma_start(out=weights[:], in_=wgs)
             nc.vector.memset(table_scales[:].bitcast(I32)[:96, :], 0)
             nc.vector.memset(table_scales[:].bitcast(I32)[96 : P - SCALE_ROWS, :], 0)
@@ -179,11 +187,14 @@ def tile_list_beacon_watch_scores_kernel(
                 return priors[s, first // BANK][:, first % BANK : first % BANK + width]
             return priors[s][:, first : first + width]
 
+        def first_bank(s):
+            return 4 if s == 1 else 0
+
         def detect(s, half):
             cols = slice(half * BANK, (half + 1) * BANK)
             rows = slice(s * P, (s + 1) * P)
             nc.tensor.matmul_mx(
-                out=banks[half][:],
+                out=banks[first_bank(s) + half][:],
                 lhsT=w1_codes[:, rows].bitcast(E4M3),
                 lhsT_scale=w1_scales[:, rows],
                 rhs=v_codes[:, cols].bitcast(E4M3),
@@ -192,7 +203,7 @@ def tile_list_beacon_watch_scores_kernel(
                 stop=True,
             )
             nc.tensor.matmul_mx(
-                out=banks[2 + half][:],
+                out=banks[first_bank(s) + 2 + half][:],
                 lhsT=w2_codes[:, 2 * s * P : 2 * (s + 1) * P].bitcast(E2M1),
                 lhsT_scale=w2_plane[:, rows],
                 rhs=v_codes[:, cols].bitcast(E4M3),
@@ -200,11 +211,14 @@ def tile_list_beacon_watch_scores_kernel(
                 start=True,
                 stop=True,
             )
-            nc.scalar.copy(out=timing[s % 2][:, cols], in_=banks[half][:])
+            nc.scalar.copy(out=timing[s % 2][:, cols], in_=banks[first_bank(s) + half][:])
+
+        def evidence_of(s):
+            return first_evidence if s == 0 else evidence[s % 3]
 
         def stronger(s, half):
             cols = slice(half * BANK, (half + 1) * BANK)
-            nc.vector.tensor_tensor(evidence[s % 3][:, cols], banks[2 + half][:], timing[s % 2][:, cols], MAX)
+            nc.vector.tensor_tensor(evidence_of(s)[:, cols], banks[2 + half][:], timing[s % 2][:, cols], MAX)
 
         def turn_add(bank_cols, sources):
             blocks = sources[0].shape[1] // P
@@ -221,11 +235,12 @@ def tile_list_beacon_watch_scores_kernel(
 
         def excess_begin(s, half):
             cols = slice(half * BANK, (half + 1) * BANK)
-            nc.scalar.activation(out=minus_volume[:, cols], in_=banks[2 + half][:], func=COPY, scale=-1.0)
-            turn_add(banks[half][:], [timing[s % 2][:, cols], minus_volume[:, cols]])
-            turn_add(banks[2 + half][:], [minus_volume[:, cols]])
-            nc.scalar.activation(out=excess_t[s][:, cols], in_=banks[half][:], func=RELU)
-            nc.scalar.activation(out=volume_t[s][:, cols], in_=banks[2 + half][:], func=COPY, scale=-1.0)
+            timing_bank, volume_bank = banks[first_bank(s) + half], banks[first_bank(s) + 2 + half]
+            nc.scalar.activation(out=minus_volume[:, cols], in_=volume_bank[:], func=COPY, scale=-1.0)
+            turn_add(timing_bank[:], [timing[s % 2][:, cols], minus_volume[:, cols]])
+            turn_add(volume_bank[:], [minus_volume[:, cols]])
+            nc.scalar.activation(out=excess_t[s][:, cols], in_=timing_bank[:], func=RELU)
+            nc.scalar.activation(out=volume_t[s][:, cols], in_=volume_bank[:], func=COPY, scale=-1.0)
 
         def excess_end(s):
             last = S - LATE if s == SLICES - 1 else S
@@ -241,7 +256,7 @@ def tile_list_beacon_watch_scores_kernel(
             cols = slice(first, first + width)
             nc.vector.tensor_tensor(
                 pages[s % PAGES][:].indirect(idx2[:, first // LIST_ROWS : (first + width) // LIST_ROWS]),
-                evidence[s % 3][:, cols] if source is None else source,
+                evidence_of(s)[:, cols] if source is None else source,
                 weights[:, cols],
                 MULT,
             )
@@ -310,9 +325,7 @@ def tile_list_beacon_watch_scores_kernel(
             )
 
         quantize(first_grouped[:], w1_codes[:, : W1_CHUNKS[0]], w1_scales[:, : W1_CHUNKS[0]])
-        raw_second = load_w1(1)
         raw_third = load_w1(2)
-        nc.sync.dma_start(idx3[:], offs3)
         make_identity(nc, ident[:])
         pages = [keep.tile([P, T2], F32, name=f"page{i}", tag=f"page{i}", align_bytes=64) for i in range(PAGES - 1)]
         nc.vector.memset(pages[1][:], 0.0)
@@ -321,18 +334,16 @@ def tile_list_beacon_watch_scores_kernel(
             entries = idx[:, half * BANK // LIST_ROWS : (half + 1) * BANK // LIST_ROWS]
             cols = slice(half * BANK, (half + 1) * BANK)
             nc.vector.tensor_copy(v_codes[:, cols], table[:].bitcast(U32).indirect(entries))
-        pages.append(keep.tile([P, T2], F32, name="page2", tag="page2", align_bytes=64))
-        nc.gpsimd.memset(pages[2][:], 0.0)
-        quantize_w1(1, raw_second, "early1")
-        quantize_w1(2, raw_third, "early2")
+        round_into(second_grouped[:], raw_second)
+        second = slice(w1_first[1], w1_first[2])
+        quantize(second_grouped[:], w1_codes[:, second], w1_scales[:, second])
         for half in range(2):
             detect(0, half)
             stronger(0, half)
         scatter(0, 0, BANK)
-        for half in range(2):
-            detect(1, half)
-            stronger(1, half)
         scatter(0, BANK, BANK)
+        pages.append(keep.tile([P, T2], F32, name="page2", tag="page2", align_bytes=64))
+        nc.gpsimd.memset(pages[2][:], 0.0)
 
         partial = stage.tile([P, OUT_TILES, BANK], F32)
         turned = {}
@@ -374,6 +385,9 @@ def tile_list_beacon_watch_scores_kernel(
                     for pair in range(2):
                         turn_back(turned[g, half], 2 * pair, 2, banks[6 + pair], whole, nc.scalar.copy)
 
+        first_stage_begin(1)
+        excess_end(1)
+        quantize_w1(2, raw_third, "early2")
         first_stage_begin(2)
         excess_end(2)
         load_prior(0)
@@ -396,16 +410,16 @@ def tile_list_beacon_watch_scores_kernel(
             if s == PACK - 1:
                 z_codes[0] = stage.tile([P, M], U32, name="z_codes0", align_bytes=64)
                 quantize_z(0, packed[0][:], 0, M)
-            if s + 2 < SLICES:
-                load_prior(s + 2)
-        second_codes = stage.tile([P, BANK], U32, name="z_codes1", tag="excess1", align_bytes=64)
-        z_codes[1, 1] = second_codes[:]
-        quantize_z(1, packed[1][:, BANK * PACK :], BANK, BANK)
-        for nt in range(OUT_TILES):
-            bank = banks[6 + nt % 2]
-            for early in range(GROUPS - 1):
-                score_pass(bank[:], nt, early, BANK, early == 0, early == GROUPS - 2)
-            nc.scalar.copy(out=partial[:, nt, :], in_=bank[:])
+            if s == SLICES - 4:
+                second_codes = stage.tile([P, BANK], U32, name="z_codes1", tag="excess1", align_bytes=64)
+                z_codes[1, 1] = second_codes[:]
+                quantize_z(1, packed[1][:, BANK * PACK :], BANK, BANK)
+                for nt in range(OUT_TILES):
+                    bank = banks[6 + nt % 2]
+                    for early in range(GROUPS - 1):
+                        score_pass(bank[:], nt, early, BANK, early == 0, early == GROUPS - 2)
+                    nc.scalar.copy(out=partial[:, nt, :], in_=bank[:])
+            load_prior(s + 2)
         z_codes[GROUPS - 1] = stage.tile([P, M], U32, name="z_codes_last", align_bytes=64)
         s = SLICES - 2
         scatter(s + 1, 0, S - LATE)

@@ -60,9 +60,10 @@ def tile_list_beacon_watch_scores_kernel(
         idx2 = keep.tile([P, S // LIST_ROWS], U16)
         idx3 = keep.tile([P, M // LIST_ROWS], U16)
         table = keep.tile([P, T], I32, align_bytes=64)
+        first_timing = keep.tile([P, BANK], F32, tag="page1", align_bytes=64)
         first_evidence = keep.tile([P, S], F32, tag="page2", align_bytes=64)
         table_scales = keep.tile([P, T], U8, tag="page0", align_bytes=64)
-        w2_codes = keep.tile([P, 2 * H], U8, align_bytes=64)
+        w2_first = keep.tile([P, 4 * P], U8, align_bytes=64)
         weights = keep.tile([P, S], F32)
         v_codes = keep.tile([P, S], U32, align_bytes=64)
         v_scales = keep.tile([P, S], U8, align_bytes=64)
@@ -103,14 +104,14 @@ def tile_list_beacon_watch_scores_kernel(
             first_raw = head.tile([P, PACK, W1_CHUNKS[0]], F32)
             load_into(first_raw, w1[:, : W1_CHUNKS[0]])
             w2_rows = w2_words[0].bitcast(I32)
-            first_words = P // 2
-            nc.sync.dma_start(out=w2_codes[:].bitcast(I32)[:, :first_words], in_=w2_rows[:, :first_words])
+            first_words = P
+            nc.sync.dma_start(out=w2_first[:].bitcast(I32), in_=w2_rows[:, :first_words])
             nc.sync.dma_start(idx2[:], offs2)
             nc.sync.dma_start(idx3[:], offs3)
             nc.sync.dma_start(out=table[:], in_=tab_words[0].rearrange("p t i -> p (t i)").bitcast(I32))
-            nc.sync.dma_start(out=w2_codes[:].bitcast(I32)[:, first_words:], in_=w2_rows[:, first_words:])
+            nc.sync.dma_start(out=weights[:, :BANK], in_=wgs[:, :BANK])
             load_into(raw_second, w1[:, W1_CHUNKS[0] : W1_CHUNKS[0] + W1_CHUNKS[1]])
-            nc.sync.dma_start(out=weights[:], in_=wgs)
+            nc.sync.dma_start(out=weights[:, BANK:], in_=wgs[:, BANK:])
             nc.vector.memset(table_scales[:].bitcast(I32)[:96, :], 0)
             nc.vector.memset(table_scales[:].bitcast(I32)[96 : P - SCALE_ROWS, :], 0)
             nc.vector.memset(v_scales[:].bitcast(I32), 0)
@@ -187,6 +188,11 @@ def tile_list_beacon_watch_scores_kernel(
                 return priors[s, first // BANK][:, first % BANK : first % BANK + width]
             return priors[s][:, first : first + width]
 
+        def timing_of(s, half):
+            if (s, half) == (0, 0):
+                return first_timing[:]
+            return timing[s % 2][:, half * BANK : (half + 1) * BANK]
+
         def first_bank(s):
             return 4 if s == 1 else 0
 
@@ -204,21 +210,23 @@ def tile_list_beacon_watch_scores_kernel(
             )
             nc.tensor.matmul_mx(
                 out=banks[first_bank(s) + 2 + half][:],
-                lhsT=w2_codes[:, 2 * s * P : 2 * (s + 1) * P].bitcast(E2M1),
+                lhsT=(
+                    w2_first[:, 2 * s * P : 2 * (s + 1) * P] if s < 2 else w2_rest[:, 2 * (s - 2) * P : 2 * (s - 1) * P]
+                ).bitcast(E2M1),
                 lhsT_scale=w2_plane[:, rows],
                 rhs=v_codes[:, cols].bitcast(E4M3),
                 rhs_scale=v_scales[:, cols],
                 start=True,
                 stop=True,
             )
-            nc.scalar.copy(out=timing[s % 2][:, cols], in_=banks[first_bank(s) + half][:])
+            nc.scalar.copy(out=timing_of(s, half), in_=banks[first_bank(s) + half][:])
 
         def evidence_of(s):
             return first_evidence if s == 0 else evidence[s % 3]
 
         def stronger(s, half):
             cols = slice(half * BANK, (half + 1) * BANK)
-            nc.vector.tensor_tensor(evidence_of(s)[:, cols], banks[2 + half][:], timing[s % 2][:, cols], MAX)
+            nc.vector.tensor_tensor(evidence_of(s)[:, cols], banks[2 + half][:], timing_of(s, half), MAX)
 
         def turn_add(bank_cols, sources):
             blocks = sources[0].shape[1] // P
@@ -237,7 +245,7 @@ def tile_list_beacon_watch_scores_kernel(
             cols = slice(half * BANK, (half + 1) * BANK)
             timing_bank, volume_bank = banks[first_bank(s) + half], banks[first_bank(s) + 2 + half]
             nc.scalar.activation(out=minus_volume[:, cols], in_=volume_bank[:], func=COPY, scale=-1.0)
-            turn_add(timing_bank[:], [timing[s % 2][:, cols], minus_volume[:, cols]])
+            turn_add(timing_bank[:], [timing_of(s, half), minus_volume[:, cols]])
             turn_add(volume_bank[:], [minus_volume[:, cols]])
             nc.scalar.activation(out=excess_t[s][:, cols], in_=timing_bank[:], func=RELU)
             nc.scalar.activation(out=volume_t[s][:, cols], in_=volume_bank[:], func=COPY, scale=-1.0)
@@ -326,24 +334,27 @@ def tile_list_beacon_watch_scores_kernel(
 
         quantize(first_grouped[:], w1_codes[:, : W1_CHUNKS[0]], w1_scales[:, : W1_CHUNKS[0]])
         raw_third = load_w1(2)
+        w2_rest = stage.tile([P, 2 * (H - 2 * P)], U8, align_bytes=64)
+        nc.sync.dma_start(out=w2_rest[:].bitcast(I32), in_=w2_rows[:, first_words:])
         make_identity(nc, ident[:])
-        pages = [keep.tile([P, T2], F32, name=f"page{i}", tag=f"page{i}", align_bytes=64) for i in range(PAGES - 1)]
-        nc.vector.memset(pages[1][:], 0.0)
+        pages = [keep.tile([P, T2], F32, name="page0", tag="page0", align_bytes=64)]
         nc.vector.memset(pages[0][:], 0.0)
         for half in range(2):
             entries = idx[:, half * BANK // LIST_ROWS : (half + 1) * BANK // LIST_ROWS]
             cols = slice(half * BANK, (half + 1) * BANK)
             nc.vector.tensor_copy(v_codes[:, cols], table[:].bitcast(U32).indirect(entries))
+        detect(0, 0)
+        stronger(0, 0)
         round_into(second_grouped[:], raw_second)
         second = slice(w1_first[1], w1_first[2])
         quantize(second_grouped[:], w1_codes[:, second], w1_scales[:, second])
-        for half in range(2):
-            detect(0, half)
-            stronger(0, half)
         scatter(0, 0, BANK)
+        detect(0, 1)
+        stronger(0, 1)
         scatter(0, BANK, BANK)
-        pages.append(keep.tile([P, T2], F32, name="page2", tag="page2", align_bytes=64))
-        nc.gpsimd.memset(pages[2][:], 0.0)
+        for i in range(1, PAGES):
+            pages.append(keep.tile([P, T2], F32, name=f"page{i}", tag=f"page{i}", align_bytes=64))
+            nc.gpsimd.memset(pages[i][:], 0.0)
 
         partial = stage.tile([P, OUT_TILES, BANK], F32)
         turned = {}

@@ -452,25 +452,42 @@ def tile_list_beacon_watch_scores_kernel(
         sum_at = (3, 4, 5, 4, 5)
         sum_banks = [banks[b] for b in sum_at]
         back_banks = (banks[6], banks[7], banks[3], banks[6], banks[4])
-        back_copy = (nc.scalar.copy, nc.scalar.copy, nc.vector.tensor_copy, nc.scalar.copy, nc.scalar.copy)
+        back_copy = (nc.scalar.copy, nc.vector.tensor_copy, nc.scalar.copy, nc.scalar.copy, nc.scalar.copy)
         out_rows = out.rearrange("(t p) m -> p t m", p=P)
+        wide = widths[0]
+
+        def open_sum(c, nt):
+            return banks[c][:, nt * wide : (nt + 1) * wide] if nt < 2 else banks[2][:, c * wide : (c + 1) * wide]
 
         early = len(set(sum_at))
         for c in range(early):
             turn_terms(sum_banks[c][:], priors[s][:, firsts[c] : firsts[c] + widths[c]], True, False)
-        for nt in range(OUT_TILES):
-            for step in range(GROUPS - 1):
-                score_pass(banks[nt][:], nt, GROUPS - 2 - step, 0, step == 0, False)
+        for step in range(GROUPS - 1):
+            for c in range(2):
+                for nt in range(OUT_TILES):
+                    opens = step == 0 and (nt == 0 or (nt == 2 and c == 0))
+                    score_pass(open_sum(c, nt), nt, GROUPS - 2 - step, firsts[c], opens, False)
         for c, chunk in enumerate(widths):
             gather(s, firsts[c], chunk)
 
+        def pack(c):
+            turn_back(turned[g, c], 0, widths[c] // P, back_banks[c], packed[g, c], back_copy[c])
+            quantize_z(g, packed[g, c][:], firsts[c], widths[c])
+
+        def hand_over(name, bank, rows):
+            result = stage.tile([P, BANK], F32, name=name)
+            nc.scalar.copy(out=result[:], in_=bank[:])
+            nc.sync.dma_start(out=rows, in_=result[:].rearrange("p (t m) -> p t m", t=rows.shape[1]))
+
         def finish(c):
             first, chunk = firsts[c], widths[c]
-            turn_back(turned[g, c], 0, chunk // P, back_banks[c], packed[g, c], back_copy[c])
-            quantize_z(g, packed[g, c][:], first, chunk)
             if first < BANK:
                 for nt in range(OUT_TILES):
-                    score_pass(banks[nt][:, first : first + chunk], nt, g, first, False, first + chunk == BANK)
+                    closes = nt == 1 or (nt == 2 and c == 1)
+                    score_pass(open_sum(c, nt), nt, g, first, False, closes)
+                hand_over(f"result{c}", banks[c], out_rows[:, :2, first : first + chunk])
+                if c == 1:
+                    hand_over("result_third", banks[2], out_rows[:, 2:, :BANK])
                 return
             result = stage.tile([P, OUT_TILES, chunk], F32, name=f"result{c}")
             fits = OUT_TILES * chunk <= BANK
@@ -493,9 +510,7 @@ def tile_list_beacon_watch_scores_kernel(
             turn_terms(sum_banks[c][:], change[s][:, cols], False, True)
             round_turned(s, sum_banks[c][:, :chunk], turned[g, c])
             if c >= 1:
-                finish(c - 1)
-        finish(len(widths) - 1)
-        for nt in range(OUT_TILES):
-            first_half = stage.tile([P, BANK], F32, name="first_half", bufs=OUT_TILES)
-            nc.scalar.copy(out=first_half[:], in_=banks[nt][:])
-            nc.sync.dma_start(out=out_rows[:, nt, :BANK], in_=first_half[:])
+                pack(c - 1)
+        pack(len(widths) - 1)
+        for c in range(len(widths)):
+            finish(c)

@@ -17,7 +17,6 @@ E2M1 = mybir.dt.float4_e2m1fn_x4
 MULT = mybir.AluOpType.mult
 ADD = mybir.AluOpType.add
 MAX = mybir.AluOpType.max
-SUBTRACT = mybir.AluOpType.subtract
 COPY = mybir.ActivationFunctionType.Copy
 RELU = mybir.ActivationFunctionType.Relu
 
@@ -28,12 +27,14 @@ BANK = 512
 SLICES = H // P
 GROUPS = H // K_PASS
 OUT_TILES = N // P
+QUADRANT = 32
 SCALE_ROWS = K_PASS // 32
 LIST_ROWS = 16
 W1_CHUNKS = (128, 128, 256, 512, 256, 256)
 W3_CHUNKS = (512, 512, 128)
 W1_AFTER = {0: 4, 2: 5}
 W3_AFTER = {1: 0, 5: 1, 6: 2}
+EARLY_W2 = 2
 MAIN_CHUNKS = (512, 512)
 TAIL_CHUNKS = (256, 256, 256, 128, 128)
 LATE = 256
@@ -63,7 +64,7 @@ def tile_list_beacon_watch_scores_kernel(
         first_timing = keep.tile([P, BANK], F32, tag="page1", align_bytes=64)
         first_evidence = keep.tile([P, S], F32, tag="page2", align_bytes=64)
         table_scales = keep.tile([P, T], U8, tag="page0", align_bytes=64)
-        w2_first = keep.tile([P, 4 * P], U8, align_bytes=64)
+        w2_first = keep.tile([P, 2 * EARLY_W2 * P], U8, align_bytes=64)
         weights = keep.tile([P, S], F32)
         v_codes = keep.tile([P, S], U32, align_bytes=64)
         v_scales = keep.tile([P, S], U8, align_bytes=64)
@@ -81,11 +82,10 @@ def tile_list_beacon_watch_scores_kernel(
         minus_volume = keep.tile([P, S], F32)
         evidence = [keep.tile([P, S], F32, name=f"evidence{i}") for i in range(3)]
 
-        def load_scale_rows(queue, plane, rows):
+        def place_scale_rows(queue, plane, rows):
             for q in range(4):
                 queue.dma_start(
-                    out=plane[:].bitcast(I32)[32 * q : 32 * q + 4, :],
-                    in_=rows[0, 4 * q : 4 * q + 4, :].bitcast(I32),
+                    out=plane[:].bitcast(I32)[QUADRANT * q : QUADRANT * q + 4, :], in_=rows[4 * q : 4 * q + 4, :]
                 )
 
         def load_into(raw, rows):
@@ -104,7 +104,7 @@ def tile_list_beacon_watch_scores_kernel(
             first_raw = head.tile([P, PACK, W1_CHUNKS[0]], F32)
             load_into(first_raw, w1[:, : W1_CHUNKS[0]])
             w2_rows = w2_words[0].bitcast(I32)
-            first_words = P
+            first_words = EARLY_W2 * P // 2
             nc.sync.dma_start(out=w2_first[:].bitcast(I32), in_=w2_rows[:, :first_words])
             nc.sync.dma_start(idx2[:], offs2)
             nc.sync.dma_start(idx3[:], offs3)
@@ -112,25 +112,20 @@ def tile_list_beacon_watch_scores_kernel(
             nc.sync.dma_start(out=weights[:, :BANK], in_=wgs[:, :BANK])
             load_into(raw_second, w1[:, W1_CHUNKS[0] : W1_CHUNKS[0] + W1_CHUNKS[1]])
             nc.sync.dma_start(out=weights[:, BANK:], in_=wgs[:, BANK:])
-            nc.vector.memset(table_scales[:].bitcast(I32)[:96, :], 0)
-            nc.vector.memset(table_scales[:].bitcast(I32)[96 : P - SCALE_ROWS, :], 0)
+            nc.vector.memset(table_scales[:].bitcast(I32)[: P - QUADRANT, :], 0)
+            nc.vector.memset(table_scales[:].bitcast(I32)[P - QUADRANT : P - SCALE_ROWS, :], 0)
             nc.vector.memset(v_scales[:].bitcast(I32), 0)
             nc.gpsimd.memset(w2_plane[:].bitcast(I32), 0)
-            load_scale_rows(nc.gpsimd, w2_plane, w2_scales)
+            place_scale_rows(nc.gpsimd, w2_plane, w2_scales[0].bitcast(I32))
             nc.vector.tensor_copy(picked_scales[:], table_scales[:].indirect(idx[:]))
             round_into(first_grouped[:], first_raw)
-            for q in range(4):
-                first_row = P - SCALE_ROWS + 4 * q
-                nc.scalar.dma_start(
-                    out=v_scales[:].bitcast(I32)[32 * q : 32 * q + 4, :],
-                    in_=picked_scales[:].bitcast(I32)[first_row : first_row + 4, :],
-                )
+            place_scale_rows(nc.scalar, v_scales, picked_scales[:].bitcast(I32)[P - SCALE_ROWS :, :])
 
         stage = ctx.enter_context(tc.tile_pool(name="stage", bufs=1))
         priors, change, z_codes, excess_t, volume_t = {}, {}, {}, {}, {}
 
-        def ring_tile(name, place, width=M, dtype=F32):
-            return stage.tile([P, width], dtype, name=name, tag=f"ring{place % RING}", align_bytes=64)
+        def ring_tile(name, place):
+            return stage.tile([P, M], F32, name=name, tag=f"ring{place % RING}", align_bytes=64)
 
         def load_rows(rows):
             raw = stage.tile([P, PACK, rows.shape[1]], F32, name="raw", bufs=RAW_BUFS)
@@ -196,6 +191,10 @@ def tile_list_beacon_watch_scores_kernel(
         def first_bank(s):
             return 4 if s == 1 else 0
 
+        def w2_of(s):
+            codes, at = (w2_first, s) if s < EARLY_W2 else (w2_rest, s - EARLY_W2)
+            return codes[:, 2 * at * P : 2 * (at + 1) * P]
+
         def detect(s, half):
             cols = slice(half * BANK, (half + 1) * BANK)
             rows = slice(s * P, (s + 1) * P)
@@ -210,9 +209,7 @@ def tile_list_beacon_watch_scores_kernel(
             )
             nc.tensor.matmul_mx(
                 out=banks[first_bank(s) + 2 + half][:],
-                lhsT=(
-                    w2_first[:, 2 * s * P : 2 * (s + 1) * P] if s < 2 else w2_rest[:, 2 * (s - 2) * P : 2 * (s - 1) * P]
-                ).bitcast(E2M1),
+                lhsT=w2_of(s).bitcast(E2M1),
                 lhsT_scale=w2_plane[:, rows],
                 rhs=v_codes[:, cols].bitcast(E4M3),
                 rhs_scale=v_scales[:, cols],
@@ -224,22 +221,25 @@ def tile_list_beacon_watch_scores_kernel(
         def evidence_of(s):
             return first_evidence if s == 0 else evidence[s % 3]
 
-        def stronger(s, half):
+        def first_maximum(half):
             cols = slice(half * BANK, (half + 1) * BANK)
-            nc.vector.tensor_tensor(evidence_of(s)[:, cols], banks[2 + half][:], timing_of(s, half), MAX)
+            nc.vector.tensor_tensor(first_evidence[:, cols], banks[2 + half][:], timing_of(0, half), MAX)
+
+        def turn_terms(bank_cols, source, start, stop):
+            blocks = source.shape[1] // P
+            for b in range(blocks):
+                nc.tensor.matmul(
+                    bank_cols[:, b * P : (b + 1) * P],
+                    source[:, b * P : (b + 1) * P],
+                    ident[:],
+                    is_transpose=True,
+                    start=(start and b == 0),
+                    stop=(stop and b == blocks - 1),
+                )
 
         def turn_add(bank_cols, sources):
-            blocks = sources[0].shape[1] // P
             for term, source in enumerate(sources):
-                for b in range(blocks):
-                    nc.tensor.matmul(
-                        bank_cols[:, b * P : (b + 1) * P],
-                        source[:, b * P : (b + 1) * P],
-                        ident[:],
-                        is_transpose=True,
-                        start=(term == 0 and b == 0),
-                        stop=(term == len(sources) - 1 and b == blocks - 1),
-                    )
+                turn_terms(bank_cols, source, term == 0, term == len(sources) - 1)
 
         def excess_begin(s, half):
             cols = slice(half * BANK, (half + 1) * BANK)
@@ -277,22 +277,6 @@ def tile_list_beacon_watch_scores_kernel(
                 prior_of(s, first, width),
                 MULT,
             )
-
-        def turn_terms(bank_cols, source, start, stop):
-            blocks = source.shape[1] // P
-            for b in range(blocks):
-                nc.tensor.matmul(
-                    bank_cols[:, b * P : (b + 1) * P],
-                    source[:, b * P : (b + 1) * P],
-                    ident[:],
-                    is_transpose=True,
-                    start=(start and b == 0),
-                    stop=(stop and b == blocks - 1),
-                )
-
-        def turn_sum(s, first, width, bank):
-            cols = slice(first, first + width)
-            turn_add(bank[:, :width], [priors[s][:, cols], change[s][:, cols]])
 
         def round_turned(s, bank_cols, turned):
             place = s % PACK
@@ -334,7 +318,7 @@ def tile_list_beacon_watch_scores_kernel(
 
         quantize(first_grouped[:], w1_codes[:, : W1_CHUNKS[0]], w1_scales[:, : W1_CHUNKS[0]])
         raw_third = load_w1(2)
-        w2_rest = stage.tile([P, 2 * (H - 2 * P)], U8, align_bytes=64)
+        w2_rest = stage.tile([P, 2 * (H - EARLY_W2 * P)], U8, align_bytes=64)
         nc.sync.dma_start(out=w2_rest[:].bitcast(I32), in_=w2_rows[:, first_words:])
         make_identity(nc, ident[:])
         pages = [keep.tile([P, T2], F32, name="page0", tag="page0", align_bytes=64)]
@@ -344,13 +328,13 @@ def tile_list_beacon_watch_scores_kernel(
             cols = slice(half * BANK, (half + 1) * BANK)
             nc.vector.tensor_copy(v_codes[:, cols], table[:].bitcast(U32).indirect(entries))
         detect(0, 0)
-        stronger(0, 0)
+        first_maximum(0)
         round_into(second_grouped[:], raw_second)
         second = slice(w1_first[1], w1_first[2])
         quantize(second_grouped[:], w1_codes[:, second], w1_scales[:, second])
         scatter(0, 0, BANK)
         detect(0, 1)
-        stronger(0, 1)
+        first_maximum(1)
         scatter(0, BANK, BANK)
         for i in range(1, PAGES):
             pages.append(keep.tile([P, T2], F32, name=f"page{i}", tag=f"page{i}", align_bytes=64))
@@ -432,6 +416,7 @@ def tile_list_beacon_watch_scores_kernel(
                     nc.scalar.copy(out=partial[:, nt, :], in_=bank[:])
             load_prior(s + 2)
         z_codes[GROUPS - 1] = stage.tile([P, M], U32, name="z_codes_last", align_bytes=64)
+
         s = SLICES - 2
         scatter(s + 1, 0, S - LATE)
         change[s] = ring_tile(f"change{s}", s - 3)
@@ -459,14 +444,14 @@ def tile_list_beacon_watch_scores_kernel(
         def open_sum(c, nt):
             return banks[c][:, nt * wide : (nt + 1) * wide] if nt < 2 else banks[2][:, c * wide : (c + 1) * wide]
 
-        early = len(set(sum_at))
-        for c in range(early):
+        ahead = len(set(sum_at))
+        for c in range(ahead):
             turn_terms(sum_banks[c][:], priors[s][:, firsts[c] : firsts[c] + widths[c]], True, False)
-        for step in range(GROUPS - 1):
+        for early in range(GROUPS - 1):
             for c in range(2):
                 for nt in range(OUT_TILES):
-                    opens = step == 0 and (nt == 0 or (nt == 2 and c == 0))
-                    score_pass(open_sum(c, nt), nt, GROUPS - 2 - step, firsts[c], opens, False)
+                    opens = early == 0 and (nt == 0 or (nt == 2 and c == 0))
+                    score_pass(open_sum(c, nt), nt, early, firsts[c], opens, False)
         for c, chunk in enumerate(widths):
             gather(s, firsts[c], chunk)
 
@@ -505,7 +490,7 @@ def tile_list_beacon_watch_scores_kernel(
 
         for c, chunk in enumerate(widths):
             cols = slice(firsts[c], firsts[c] + chunk)
-            if c >= early:
+            if c >= ahead:
                 turn_terms(sum_banks[c][:], priors[s][:, cols], True, False)
             turn_terms(sum_banks[c][:], change[s][:, cols], False, True)
             round_turned(s, sum_banks[c][:, :chunk], turned[g, c])

from contextlib import ExitStack

import concourse.mybir as mybir
from concourse.masks import make_identity

K, T, S, H, T2, M, N = 512, 4096, 1024, 1536, 2048, 1024, 384
FLOPS = 2 * (2 * K * H * S + H * N * M)

F32 = mybir.dt.float32
BF16 = mybir.dt.bfloat16
I32 = mybir.dt.int32
U32 = mybir.dt.uint32
U16 = mybir.dt.uint16
U8 = mybir.dt.uint8
E4M3 = mybir.dt.float8_e4m3fn_x4
E2M1 = mybir.dt.float4_e2m1fn_x4
MULT = mybir.AluOpType.mult
ADD = mybir.AluOpType.add
MAX = mybir.AluOpType.max
COPY = mybir.ActivationFunctionType.Copy
RELU = mybir.ActivationFunctionType.Relu

P = 128
PACK = 4
K_PASS = P * PACK
BANK = 512
SLICES = H // P
GROUPS = H // K_PASS
OUT_TILES = N // P
QUADRANT = 32
SCALE_ROWS = K_PASS // 32
LIST_ROWS = 16
W1_CHUNKS = (128, 128, 256, 512, 256, 256)
W3_CHUNKS = (512, 512, 128)
W1_AFTER = {0: 4, 2: 5}
W3_AFTER = {1: 0, 5: 1, 6: 2}
EARLY_W2 = 2
MAIN_CHUNKS = (512, 512)
TAIL_CHUNKS = (256, 256, 256, 128, 128)
LATE = 256
PAGES = 3
RING = 5
RAW_BUFS = 3


def starts(widths):
    return [sum(widths[:c]) for c in range(len(widths))]


def tile_list_beacon_watch_scores_kernel(
    tc, tab_words, tab_scales, offs, offs2, offs3, w1, w2_words, w2_scales, wgs, prior, w3, out
):
    nc = tc.nc
    with ExitStack() as ctx:
        keep = ctx.enter_context(tc.tile_pool(name="keep", bufs=1))
        psum = ctx.enter_context(tc.psum_pool(name="psum", bufs=1))

        banks = [psum.tile([P, BANK], F32, name=f"bank{b}") for b in range(8)]

        idx = keep.tile([P, S // LIST_ROWS], U16)
        idx2 = keep.tile([P, S // LIST_ROWS], U16)
        idx3 = keep.tile([P, M // LIST_ROWS], U16)
        table = keep.tile([P, T], I32, align_bytes=64)
        first_timing = keep.tile([P, BANK], F32, tag="page1", align_bytes=64)
        first_evidence = keep.tile([P, S], F32, tag="page2", align_bytes=64)
        table_scales = keep.tile([P, T], U8, tag="page0", align_bytes=64)
        w2_first = keep.tile([P, 2 * EARLY_W2 * P], U8, align_bytes=64)
        weights = keep.tile([P, S], F32)
        v_codes = keep.tile([P, S], U32, align_bytes=64)
        v_scales = keep.tile([P, S], U8, align_bytes=64)
        w1_codes = keep.tile([P, H], U32, align_bytes=64)
        w1_scales = keep.tile([P, H], U8, align_bytes=64)
        w2_plane = keep.tile([P, H], U8, align_bytes=64)
        w3_codes = keep.tile([P, GROUPS * N], U32, align_bytes=64)
        w3_scales = keep.tile([P, GROUPS * N], U8, align_bytes=64)
        z_scales = keep.tile([P, GROUPS * M], U8, align_bytes=64)
        first_grouped = keep.tile([P, W1_CHUNKS[0] * PACK], BF16, align_bytes=64)
        raw_second = keep.tile([P, PACK, W1_CHUNKS[1]], F32)
        second_grouped = keep.tile([P, W1_CHUNKS[1] * PACK], BF16, align_bytes=64)
        ident = keep.tile([P, P], F32)
        timing = [keep.tile([P, S], F32, name=f"timing{i}") for i in range(2)]
        minus_volume = keep.tile([P, S], F32)
        evidence = [keep.tile([P, S], F32, name=f"evidence{i}") for i in range(3)]

        def place_scale_rows(queue, plane, rows):
            for q in range(4):
                queue.dma_start(
                    out=plane[:].bitcast(I32)[QUADRANT * q : QUADRANT * q + 4, :], in_=rows[4 * q : 4 * q + 4, :]
                )

        def load_into(raw, rows):
            nc.sync.dma_start(out=raw[:], in_=rows.rearrange("(p j) c -> p j c", j=PACK))

        def round_into(grouped, raw):
            nc.scalar.copy(
                out=grouped.rearrange("p (c i j) -> p c j i", i=4, j=PACK),
                in_=raw[:].rearrange("p j (c i) -> p c j i", i=4),
            )

        nc.sync.dma_start(idx[:], offs)
        with tc.tile_pool(name="head", bufs=1) as head:
            picked_scales = head.tile([P, S], U8, align_bytes=64)
            nc.sync.dma_start(out=table_scales[:].bitcast(I32)[P - SCALE_ROWS :, :], in_=tab_scales[0].bitcast(I32))
            first_raw = head.tile([P, PACK, W1_CHUNKS[0]], F32)
            load_into(first_raw, w1[:, : W1_CHUNKS[0]])
            w2_rows = w2_words[0].bitcast(I32)
            first_words = EARLY_W2 * P // 2
            nc.sync.dma_start(out=w2_first[:].bitcast(I32), in_=w2_rows[:, :first_words])
            nc.sync.dma_start(idx2[:], offs2)
            nc.sync.dma_start(idx3[:], offs3)
            nc.sync.dma_start(out=table[:], in_=tab_words[0].rearrange("p t i -> p (t i)").bitcast(I32))
            nc.sync.dma_start(out=weights[:, :BANK], in_=wgs[:, :BANK])
            load_into(raw_second, w1[:, W1_CHUNKS[0] : W1_CHUNKS[0] + W1_CHUNKS[1]])
            nc.sync.dma_start(out=weights[:, BANK:], in_=wgs[:, BANK:])
            nc.vector.memset(table_scales[:].bitcast(I32)[: P - QUADRANT, :], 0)
            nc.vector.memset(table_scales[:].bitcast(I32)[P - QUADRANT : P - SCALE_ROWS, :], 0)
            nc.vector.memset(v_scales[:].bitcast(I32), 0)
            nc.gpsimd.memset(w2_plane[:].bitcast(I32), 0)
            place_scale_rows(nc.gpsimd, w2_plane, w2_scales[0].bitcast(I32))
            nc.vector.tensor_copy(picked_scales[:], table_scales[:].indirect(idx[:]))
            round_into(first_grouped[:], first_raw)
            place_scale_rows(nc.scalar, v_scales, picked_scales[:].bitcast(I32)[P - SCALE_ROWS :, :])

        stage = ctx.enter_context(tc.tile_pool(name="stage", bufs=1))
        priors, change, z_codes, excess_t, volume_t = {}, {}, {}, {}, {}

        def ring_tile(name, place):
            return stage.tile([P, M], F32, name=name, tag=f"ring{place % RING}", align_bytes=64)

        def load_rows(rows):
            raw = stage.tile([P, PACK, rows.shape[1]], F32, name="raw", bufs=RAW_BUFS)
            load_into(raw, rows)
            return raw

        def quantize(grouped, codes, scales):
            nc.vector.quantize_mx(out=codes.bitcast(E4M3), scales=scales, in_=grouped)

        w1_first = starts(W1_CHUNKS)

        def load_w1(c):
            return load_rows(w1[:, w1_first[c] : w1_first[c] + W1_CHUNKS[c]])

        def quantize_w1(c, raw, tag):
            grouped = stage.tile([P, W1_CHUNKS[c] * PACK], BF16, name=f"w1_grouped{c}", tag=tag, align_bytes=64)
            round_into(grouped[:], raw)
            cols = slice(w1_first[c], w1_first[c] + W1_CHUNKS[c])
            quantize(grouped[:], w1_codes[:, cols], w1_scales[:, cols])

        w3_first = starts(W3_CHUNKS)

        def quantize_w3(c, tag):
            first, width = w3_first[c], W3_CHUNKS[c]
            grouped = stage.tile([P, width * PACK], BF16, name=f"w3_grouped{c}", tag=tag, align_bytes=64)
            for g in range(GROUPS):
                lo, hi = max(first, g * N), min(first + width, (g + 1) * N)
                if lo < hi:
                    raw = load_rows(w3[g * K_PASS : (g + 1) * K_PASS, lo - g * N : hi - g * N])
                    round_into(grouped[:, (lo - first) * PACK : (hi - first) * PACK], raw)
            quantize(grouped[:], w3_codes[:, first : first + width], w3_scales[:, first : first + width])

        def codes_of(g, first, width):
            half, at = divmod(first, BANK)
            if (g, half) in z_codes:
                return z_codes[g, half][:, at : at + width]
            return z_codes[g][:, first : first + width]

        def quantize_z(g, grouped, first, width):
            quantize(grouped, codes_of(g, first, width), z_scales[:, g * M + first : g * M + first + width])

        def load_prior(s):
            if s == SLICES - 2:
                for half, tag in enumerate((f"ring{s % RING}", "volume1")):
                    priors[s, half] = stage.tile([P, BANK], F32, name=f"prior{s}_{half}", tag=tag, align_bytes=64)
                    nc.sync.dma_start(
                        out=priors[s, half][:], in_=prior[s * P : (s + 1) * P, half * BANK : (half + 1) * BANK]
                    )
                return
            priors[s] = ring_tile(f"prior{s}", s)
            nc.sync.dma_start(out=priors[s][:], in_=prior[s * P : (s + 1) * P, :])

        def prior_of(s, first, width):
            if s == SLICES - 2:
                return priors[s, first // BANK][:, first % BANK : first % BANK + width]
            return priors[s][:, first : first + width]

        def timing_of(s, half):
            if (s, half) == (0, 0):
                return first_timing[:]
            return timing[s % 2][:, half * BANK : (half + 1) * BANK]

        def first_bank(s):
            return 4 if s == 1 else 0

        def w2_of(s):
            codes, at = (w2_first, s) if s < EARLY_W2 else (w2_rest, s - EARLY_W2)
            return codes[:, 2 * at * P : 2 * (at + 1) * P]

        def detect(s, half):
            cols = slice(half * BANK, (half + 1) * BANK)
            rows = slice(s * P, (s + 1) * P)
            nc.tensor.matmul_mx(
                out=banks[first_bank(s) + half][:],
                lhsT=w1_codes[:, rows].bitcast(E4M3),
                lhsT_scale=w1_scales[:, rows],
                rhs=v_codes[:, cols].bitcast(E4M3),
                rhs_scale=v_scales[:, cols],
                start=True,
                stop=True,
            )
            nc.tensor.matmul_mx(
                out=banks[first_bank(s) + 2 + half][:],
                lhsT=w2_of(s).bitcast(E2M1),
                lhsT_scale=w2_plane[:, rows],
                rhs=v_codes[:, cols].bitcast(E4M3),
                rhs_scale=v_scales[:, cols],
                start=True,
                stop=True,
            )
            nc.scalar.copy(out=timing_of(s, half), in_=banks[first_bank(s) + half][:])

        def evidence_of(s):
            return first_evidence if s == 0 else evidence[s % 3]

        def first_maximum(half):
            cols = slice(half * BANK, (half + 1) * BANK)
            nc.vector.tensor_tensor(first_evidence[:, cols], banks[2 + half][:], timing_of(0, half), MAX)

        def turn_terms(bank_cols, source, start, stop):
            blocks = source.shape[1] // P
            for b in range(blocks):
                nc.tensor.matmul(
                    bank_cols[:, b * P : (b + 1) * P],
                    source[:, b * P : (b + 1) * P],
                    ident[:],
                    is_transpose=True,
                    start=(start and b == 0),
                    stop=(stop and b == blocks - 1),
                )

        def turn_add(bank_cols, sources):
            for term, source in enumerate(sources):
                turn_terms(bank_cols, source, term == 0, term == len(sources) - 1)

        def excess_begin(s, half):
            cols = slice(half * BANK, (half + 1) * BANK)
            timing_bank, volume_bank = banks[first_bank(s) + half], banks[first_bank(s) + 2 + half]
            nc.scalar.activation(out=minus_volume[:, cols], in_=volume_bank[:], func=COPY, scale=-1.0)
            turn_add(timing_bank[:], [timing_of(s, half), minus_volume[:, cols]])
            turn_add(volume_bank[:], [minus_volume[:, cols]])
            nc.scalar.activation(out=excess_t[s][:, cols], in_=timing_bank[:], func=RELU)
            nc.scalar.activation(out=volume_t[s][:, cols], in_=volume_bank[:], func=COPY, scale=-1.0)

        def excess_end(s):
            last = S - LATE if s == SLICES - 1 else S
            for half in range(2):
                cols = slice(half * BANK, min((half + 1) * BANK, last))
                bank_cols = banks[4 + half][:, : cols.stop - cols.start]
                turn_add(bank_cols, [excess_t[s][:, cols], volume_t[s][:, cols]])
                nc.scalar.copy(out=evidence[s % 3][:, cols], in_=bank_cols)
            if last < S:
                turn_add(banks[3][:, :LATE], [excess_t[s][:, last:], volume_t[s][:, last:]])

        def scatter(s, first, width, source=None):
            cols = slice(first, first + width)
            nc.vector.tensor_tensor(
                pages[s % PAGES][:].indirect(idx2[:, first // LIST_ROWS : (first + width) // LIST_ROWS]),
                evidence_of(s)[:, cols] if source is None else source,
                weights[:, cols],
                MULT,
            )

        def gather(s, first, width):
            cols = slice(first, first + width)
            nc.vector.tensor_tensor(
                change[s][:, cols],
                pages[s % PAGES][:].indirect(idx3[:, first // LIST_ROWS : (first + width) // LIST_ROWS]),
                prior_of(s, first, width),
                MULT,
            )

        def round_turned(s, bank_cols, turned):
            place = s % PACK
            nc.scalar.copy(
                out=turned[:].rearrange("m (b u p e) -> m u b p e", u=2, p=P, e=2)[
                    :, :, :, 32 * place : 32 * place + 32, :
                ],
                in_=bank_cols.rearrange("m (b p u e) -> m u b p e", p=32, u=2, e=2),
            )

        def turn_back(turned, first_block, blocks, bank, packed, engine_copy):
            for b in range(blocks):
                for u in range(2):
                    at = (first_block + b) * K_PASS + u * 2 * P
                    nc.tensor.transpose(
                        bank[:, (2 * b + u) * P : (2 * b + u + 1) * P],
                        turned[:, at : at + 2 * P].bitcast(F32),
                        ident[:],
                    )
            engine_copy(
                out=packed[:, first_block * K_PASS : (first_block + blocks) * K_PASS]
                .bitcast(F32)
                .rearrange("p (b m u) -> p b m u", b=blocks, u=2),
                in_=bank[:, : blocks * 2 * P].rearrange("p (b u m) -> p b m u", b=blocks, u=2),
            )

        def score_pass(bank_cols, nt, g, first, start, stop):
            w_cols = slice(g * N + nt * P, g * N + (nt + 1) * P)
            z_cols = slice(g * M + first, g * M + first + bank_cols.shape[1])
            nc.tensor.matmul_mx(
                out=bank_cols,
                lhsT=w3_codes[:, w_cols].bitcast(E4M3),
                lhsT_scale=w3_scales[:, w_cols],
                rhs=codes_of(g, first, bank_cols.shape[1]).bitcast(E4M3),
                rhs_scale=z_scales[:, z_cols],
                start=start,
                stop=stop,
            )

        quantize(first_grouped[:], w1_codes[:, : W1_CHUNKS[0]], w1_scales[:, : W1_CHUNKS[0]])
        raw_third = load_w1(2)
        w2_rest = stage.tile([P, 2 * (H - EARLY_W2 * P)], U8, align_bytes=64)
        nc.sync.dma_start(out=w2_rest[:].bitcast(I32), in_=w2_rows[:, first_words:])
        make_identity(nc, ident[:])
        pages = [keep.tile([P, T2], F32, name="page0", tag="page0", align_bytes=64)]
        nc.vector.memset(pages[0][:], 0.0)
        for half in range(2):
            entries = idx[:, half * BANK // LIST_ROWS : (half + 1) * BANK // LIST_ROWS]
            cols = slice(half * BANK, (half + 1) * BANK)
            nc.vector.tensor_copy(v_codes[:, cols], table[:].bitcast(U32).indirect(entries))
        detect(0, 0)
        first_maximum(0)
        round_into(second_grouped[:], raw_second)
        second = slice(w1_first[1], w1_first[2])
        quantize(second_grouped[:], w1_codes[:, second], w1_scales[:, second])
        scatter(0, 0, BANK)
        detect(0, 1)
        first_maximum(1)
        scatter(0, BANK, BANK)
        for i in range(1, PAGES):
            pages.append(keep.tile([P, T2], F32, name=f"page{i}", tag=f"page{i}", align_bytes=64))
            nc.gpsimd.memset(pages[i][:], 0.0)

        partial = stage.tile([P, OUT_TILES, BANK], F32)
        turned = {}
        packed = {}

        def first_stage_begin(s):
            excess_t[s] = stage.tile([P, S], F32, name=f"excess_t{s}", tag=f"excess{s % 2}", align_bytes=64)
            volume_t[s] = stage.tile([P, S], F32, name=f"volume_t{s}", tag=f"volume{s % 2}", align_bytes=64)
            for half in range(2):
                detect(s, half)
                excess_begin(s, half)

        def second_stage(s, between=None):
            g, place = divmod(s, PACK)
            widths = TAIL_CHUNKS if g == GROUPS - 1 else MAIN_CHUNKS
            firsts = starts(widths)
            if place == 0:
                for c, chunk in enumerate(widths):
                    tag = f"{len(widths)}_{c}"
                    turned[g, c] = stage.tile([P, chunk * PACK], BF16, name="turned" + tag, align_bytes=64)
                    if g == GROUPS - 1:
                        packed[g, c] = stage.tile([P, chunk * PACK], BF16, name="packed" + tag, align_bytes=64)
            bank0 = 6 if s == SLICES - 2 else 4
            for half in range(2):
                turn_terms(banks[bank0 + half][:], prior_of(s, half * BANK, BANK), True, False)
            if between is not None:
                between()
            for half in range(2):
                bank = banks[bank0 + half]
                turn_terms(bank[:], change[s][:, half * BANK : (half + 1) * BANK], False, True)
                for c, chunk in enumerate(widths):
                    if firsts[c] // BANK == half:
                        at = firsts[c] % BANK
                        round_turned(s, bank[:, at : at + chunk], turned[g, c])
            if place == PACK - 1:
                packed[g] = stage.tile([P, M * PACK], BF16, name="packed", align_bytes=64)
                for half in range(2):
                    whole = packed[g][:, half * BANK * PACK : (half + 1) * BANK * PACK]
                    for pair in range(2):
                        turn_back(turned[g, half], 2 * pair, 2, banks[6 + pair], whole, nc.scalar.copy)

        first_stage_begin(1)
        excess_end(1)
        quantize_w1(2, raw_third, "early2")
        first_stage_begin(2)
        excess_end(2)
        load_prior(0)
        quantize_w1(3, load_w1(3), "early3")
        first_stage_begin(3)
        load_prior(1)
        for s in range(SLICES - 2):
            scatter(s + 1, 0, S)
            change[s] = ring_tile(f"change{s}", s - 2)
            gather(s, 0, M)
            if s + 3 < SLICES:
                excess_end(s + 3)
            if s + 4 < SLICES:
                first_stage_begin(s + 4)
            second_stage(s)
            if s in W1_AFTER:
                quantize_w1(W1_AFTER[s], load_w1(W1_AFTER[s]), f"late{s}")
            if s in W3_AFTER:
                quantize_w3(W3_AFTER[s], f"late{s}")
            if s == PACK - 1:
                z_codes[0] = stage.tile([P, M], U32, name="z_codes0", align_bytes=64)
                quantize_z(0, packed[0][:], 0, M)
            if s == SLICES - 4:
                second_codes = stage.tile([P, BANK], U32, name="z_codes1", tag="excess1", align_bytes=64)
                z_codes[1, 1] = second_codes[:]
                quantize_z(1, packed[1][:, BANK * PACK :], BANK, BANK)
                for nt in range(OUT_TILES):
                    bank = banks[6 + nt % 2]
                    for early in range(GROUPS - 1):
                        score_pass(bank[:], nt, early, BANK, early == 0, early == GROUPS - 2)
                    nc.scalar.copy(out=partial[:, nt, :], in_=bank[:])
            load_prior(s + 2)
        z_codes[GROUPS - 1] = stage.tile([P, M], U32, name="z_codes_last", align_bytes=64)

        s = SLICES - 2
        scatter(s + 1, 0, S - LATE)
        change[s] = ring_tile(f"change{s}", s - 3)
        gather(s, BANK, LATE)
        gather(s, 0, BANK)
        gather(s, BANK + LATE, BANK - LATE)
        late = priors[s, 1][:, :LATE]
        second_stage(s, lambda: nc.scalar.copy(out=late, in_=banks[3][:, :LATE]))
        first_codes = stage.tile([P, BANK], U32, name="z_codes1_first", tag=f"ring{s % RING}", align_bytes=64)
        z_codes[1, 0] = first_codes[:]
        quantize_z(1, packed[1][:, : BANK * PACK], 0, BANK)
        scatter(s + 1, S - LATE, LATE, late)
        change[SLICES - 1] = ring_tile("change_last", SLICES - 3)
        widths = TAIL_CHUNKS
        firsts = starts(widths)

        s, g = SLICES - 1, GROUPS - 1
        sum_at = (3, 4, 5, 4, 5)
        sum_banks = [banks[b] for b in sum_at]
        back_banks = (banks[6], banks[7], banks[3], banks[6], banks[4])
        back_copy = (nc.scalar.copy, nc.vector.tensor_copy, nc.scalar.copy, nc.scalar.copy, nc.scalar.copy)
        out_rows = out.rearrange("(t p) m -> p t m", p=P)
        wide = widths[0]

        def open_sum(c, nt):
            return banks[c][:, nt * wide : (nt + 1) * wide] if nt < 2 else banks[2][:, c * wide : (c + 1) * wide]

        ahead = len(set(sum_at))
        for c in range(ahead):
            turn_terms(sum_banks[c][:], priors[s][:, firsts[c] : firsts[c] + widths[c]], True, False)
        for early in range(GROUPS - 1):
            for c in range(2):
                for nt in range(OUT_TILES):
                    opens = early == 0 and (nt == 0 or (nt == 2 and c == 0))
                    score_pass(open_sum(c, nt), nt, early, firsts[c], opens, False)
        for c, chunk in enumerate(widths):
            gather(s, firsts[c], chunk)

        def pack(c):
            turn_back(turned[g, c], 0, widths[c] // P, back_banks[c], packed[g, c], back_copy[c])
            quantize_z(g, packed[g, c][:], firsts[c], widths[c])

        def hand_over(name, bank, rows):
            result = stage.tile([P, BANK], F32, name=name)
            nc.scalar.copy(out=result[:], in_=bank[:])
            nc.sync.dma_start(out=rows, in_=result[:].rearrange("p (t m) -> p t m", t=rows.shape[1]))

        def finish(c):
            first, chunk = firsts[c], widths[c]
            if first < BANK:
                for nt in range(OUT_TILES):
                    closes = nt == 1 or (nt == 2 and c == 1)
                    score_pass(open_sum(c, nt), nt, g, first, False, closes)
                hand_over(f"result{c}", banks[c], out_rows[:, :2, first : first + chunk])
                if c == 1:
                    hand_over("result_third", banks[2], out_rows[:, 2:, :BANK])
                return
            result = stage.tile([P, OUT_TILES, chunk], F32, name=f"result{c}")
            fits = OUT_TILES * chunk <= BANK
            runs = [(back_banks[c], 0, OUT_TILES)] if fits else [(banks[7], 0, 2), (back_banks[c], 2, 1)]
            for bank, nt0, count in runs:
                for i in range(count):
                    score_pass(bank[:, i * chunk : (i + 1) * chunk], nt0 + i, g, first, True, True)
                nc.vector.tensor_tensor(
                    result[:, nt0 : nt0 + count, :],
                    bank[:, : count * chunk].rearrange("p (t m) -> p t m", t=count),
                    partial[:, nt0 : nt0 + count, first - BANK : first - BANK + chunk],
                    ADD,
                )
            nc.sync.dma_start(out=out_rows[:, :, first : first + chunk], in_=result[:])

        for c, chunk in enumerate(widths):
            cols = slice(firsts[c], firsts[c] + chunk)
            if c >= ahead:
                turn_terms(sum_banks[c][:], priors[s][:, cols], True, False)
            turn_terms(sum_banks[c][:], change[s][:, cols], False, True)
            round_turned(s, sum_banks[c][:, :chunk], turned[g, c])
            if c >= 1:
                pack(c - 1)
        pack(len(widths) - 1)
        for c in range(len(widths)):
            finish(c)
